import numpy as np
import ml_dtypes


def mxq(x, axis, fmt="e4m3"):
    dtype, down = {"e4m3": (ml_dtypes.float8_e4m3fn, 7), "e5m2": (ml_dtypes.float8_e5m2, 14)}[fmt]
    v = np.moveaxis(np.asarray(x, np.float32).astype(ml_dtypes.bfloat16).astype(np.float64), axis, -1)
    blocks = v.reshape(v.shape[:-1] + (-1, 32))
    amax = np.abs(blocks).max(-1, keepdims=True)
    byte = np.maximum(np.where(amax > 0, np.frexp(amax)[1] - 1 + 127, 0) - down, 1)
    scale = np.exp2(byte - 127.0)
    codes = (blocks / scale).astype(np.float32).astype(dtype).astype(np.float64)
    return np.moveaxis((codes * scale).reshape(v.shape), -1, axis)


WIDE = False


def mx_kscale(k):
    if not WIDE:
        return np.ones(k)
    levels = np.array([10, -10, 5, -5, 0])
    if k % 512:
        return np.exp2(np.random.permutation(np.resize(levels, k // 32))).repeat(32)
    a = np.empty((k // 512, 16))
    for p in range(k // 512):
        a[p, :8] = np.random.permutation(np.resize(levels, 8))
        for g in range(8):
            far = levels[np.abs(levels - a[p, g]) >= 10]
            a[p, g + 8] = far[np.random.randint(len(far))]
    return np.exp2(a.ravel()).repeat(32)


def f64(x):
    return np.asarray(x).astype(np.float64)


def striped8(idx):
    return np.asarray(idx).reshape(8, -1, 16).transpose(0, 2, 1).reshape(128, -1).astype(np.uint16)


def unstriped8(offs):
    return offs.reshape(8, 16, -1).transpose(0, 2, 1).reshape(8, -1).astype(np.int64)


def pick8(x, idx, run):
    r = np.arange(len(x))
    return x[r[:, None], idx[r % (8 * run) // run]]


E2M1 = np.array([0.0, 0.5, 1.0, 1.5, 2.0, 3.0, 4.0, 6.0, -0.0, -0.5, -1.0, -1.5, -2.0, -3.0, -4.0, -6.0])


def pack_weight(w, fmt):
    k, n = w.shape
    w = f64(np.asarray(w, np.float32).astype(ml_dtypes.bfloat16)).reshape(k // 32, 32, n)
    amax = np.abs(w).max(1)
    if fmt == "e4m3":
        byte = np.frexp(amax)[1] - 1 + 127 - 7
    else:
        mant, ex = np.frexp(amax / 6.0)
        byte = np.where(mant > 0.5, ex, ex - 1) + 127
    byte = np.clip(np.where(amax > 0, byte, 1), 1, 254)
    scaled = (w * np.exp2(127.0 - byte)[:, None, :]).reshape(k, n).astype(np.float32)
    by_word = np.ascontiguousarray(scaled.reshape(k // 512, 128, 4, n).transpose(0, 1, 3, 2))
    if fmt == "e4m3":
        words = by_word.astype(ml_dtypes.float8_e4m3fn).view(np.uint8)
    else:
        c = by_word.astype(ml_dtypes.float4_e2m1fn).view(np.uint8) & 0xF
        words = (c[..., 0::2] | (c[..., 1::2] << 4)).reshape(k // 512, 128, 2 * n)
    return np.ascontiguousarray(words), np.ascontiguousarray(byte.astype(np.uint8).reshape(k // 512, 16, n))


def unpack_weight(words, scales, fmt):
    g, _, n = scales.shape
    words = np.ascontiguousarray(words).reshape(g, 128, n, -1)
    if fmt == "e4m3":
        vals = words.view(ml_dtypes.float8_e4m3fn).astype(np.float64)
    else:
        nib = np.empty((g, 128, n, 4), np.uint8)
        nib[..., 0::2] = words & 0xF
        nib[..., 1::2] = words >> 4
        vals = E2M1[nib]
    vals = vals * np.repeat(np.exp2(scales.astype(np.float64) - 127.0), 8, axis=1)[..., None]
    return vals.transpose(0, 1, 3, 2).reshape(g * 512, n)


def sigmoid(v):
    return 1.0 / (1.0 + np.exp(-v))


D, T, Q, I, E = 512, 1024, 128, 512, 512


def setup_inputs():
    n = np.random.standard_normal
    idx = np.stack([np.random.permutation(T)[:I] for _ in range(8)])
    fd = mx_kscale(D)
    ft = mx_kscale(T)
    keysp = pack_weight(n((D, T)) / fd[:, None], "e2m1")
    return {
        "query": (n((D, Q)) * 0.4 / np.sqrt(D) * fd[:, None]).astype(np.float32),
        "keys_words": keysp[0],
        "keys_scales": keysp[1],
        "fac": (np.random.uniform(8.0, 24.0, (1, T)) * ft).astype(np.float32),
        "vals": (n((T, E)) / ft[:, None]).astype(np.float32),
        "gval": (n((T, E)) / ft[:, None]).astype(np.float32),
        "offs": striped8(idx),
    }


def reference(query, keys_words, keys_scales, fac, vals, gval, offs):
    idx = unstriped8(offs)
    keysu = unpack_weight(keys_words, keys_scales, "e2m1")
    queryq = mxq(f64(query), 0, "e4m3")
    a = queryq.T @ keysu
    b = pick8(a, idx, 16)
    p = np.exp(b - np.max(b, axis=1, keepdims=True))
    w = p / np.sum(p, axis=1, keepdims=True)
    wf = np.zeros((Q, T))
    wf[np.arange(Q)[:, None], idx[np.arange(Q) % 128 // 16]] = w
    wg = wf * f64(fac)
    wt = wg.T
    wtq = mxq(wt, 0, "e4m3")
    valsq = mxq(f64(vals), 0, "e4m3")
    o = wtq.T @ valsq
    gvalq = mxq(f64(gval), 0, "e4m3")
    u = wtq.T @ gvalq
    y = o * sigmoid(u)
    return y

@@ -1,0 +1,222 @@
+from contextlib import ExitStack
+
+import concourse.mybir as mybir
+from concourse.masks import make_identity
+
+D, T, Q, SLOTS, E = 512, 1024, 128, 512, 512
+FLOPS = 2 * Q * D * T + 2 * 2 * Q * T * E
+
+F32 = mybir.dt.float32
+BF16 = mybir.dt.bfloat16
+I32 = mybir.dt.int32
+U32 = mybir.dt.uint32
+U16 = mybir.dt.uint16
+U8 = mybir.dt.uint8
+FP8X4 = mybir.dt.float8_e4m3fn_x4
+FP4X4 = mybir.dt.float4_e2m1fn_x4
+ALU = mybir.AluOpType
+ACT = mybir.ActivationFunctionType
+AXIS = mybir.AxisListType
+
+P = 128
+PACK = 4
+K_PASS = P * PACK
+PASSES = T // K_PASS
+HALF = E // 2
+SCORE_N = 256
+FIRST = 128
+LINE = 4
+
+
+def interleave(nc, engine, grouped, raw):
+    dst = grouped.rearrange("p (c i) t -> p c t i", i=LINE)
+    src = raw.rearrange("p t (c i) -> p c t i", i=LINE)
+    if engine == "v":
+        nc.vector.tensor_copy(out=dst, in_=src)
+    elif engine == "s":
+        nc.scalar.activation(out=dst, in_=src, func=ACT.Copy)
+    else:
+        nc.gpsimd.tensor_scalar(out=dst, in0=src, scalar1=1.0, scalar2=0.0, op0=ALU.mult, op1=ALU.add)
+
+
+def tile_attend_gatedvalues_heads_kernel(tc, query, keys_words, keys_scales, fac, vals, gval, offs, out):
+    nc = tc.nc
+    with ExitStack() as ctx:
+        sb = ctx.enter_context(tc.tile_pool(name="sb", bufs=1))
+        ps = ctx.enter_context(tc.psum_pool(name="ps", bufs=1))
+
+        def tile(name, shape, dtype, tag=None):
+            return sb.tile(shape, dtype, name=name, tag=tag or name, align_bytes=64)
+
+        offsets = sb.tile([P, SLOTS // 16], U16, name="offsets")
+        q_raw = tile("q_raw", [P, PACK, Q], F32)
+        k_words = tile("k_words", [P, 2 * T], U8)
+        k_scales = tile("k_scales", [P, T], U8)
+        fac_raw = tile("fac_raw", [P, PASSES, 2 * PACK], F32)
+        nc.vector.memset(k_scales[:].bitcast(U32), 0)
+        nc.sync.dma_start(out=q_raw[:], in_=query.rearrange("(p j) q -> p j q", j=PACK))
+        nc.sync.dma_start(out=k_words[:].bitcast(I32), in_=keys_words[0].bitcast(I32))
+        for quad in range(4):
+            nc.sync.dma_start(
+                out=k_scales[32 * quad : 32 * quad + 4, :].bitcast(I32),
+                in_=keys_scales[0, 4 * quad : 4 * quad + 4, :].bitcast(I32),
+            )
+        nc.sync.dma_start(offsets[:], offs)
+
+        sources = {"g": gval, "v": vals}
+        raw = {}
+
+        def load(name, g, halves):
+            rows = sources[name][K_PASS * g : K_PASS * (g + 1), :].rearrange("(p j) e -> p j e", j=PACK)
+            t = tile("raw_%s%d%d" % (name, g, halves[0]), [P, PACK, HALF * len(halves)], F32)
+            nc.sync.dma_start(out=t[:], in_=rows[:, :, HALF * halves[0] : HALF * (halves[-1] + 1)])
+            for n, h in enumerate(halves):
+                raw[name, g, h] = t[:, :, HALF * n : HALF * (n + 1)]
+
+        loads = [(n, g, [h]) for g in range(2) for n in "gv" for h in range(2)]
+        load(*loads[0])
+        load(*loads[1])
+        nc.sync.dma_start(out=fac_raw[:, :, 0:PACK], in_=fac.rearrange("o (g p j) -> p (o g) j", g=PASSES, j=PACK))
+        for item in loads[2:]:
+            load(*item)
+
+        ident = tile("ident", [P, P], F32)
+        make_identity(nc, ident[:])
+        placed = tile("placed", [P, T], F32)
+        nc.gpsimd.memset(placed[:], 0.0)
+
+        codes = {}
+        scales = {}
+
+        groups = [(("g", 0, 0),), (("g", 0, 1),), (("v", 0, 0),), (("v", 0, 1),), (("v", 1, 0),), (("g", 1, 0), ("g", 1, 1)), (("v", 1, 1),)]
+        cast_tags = {("v", 0, 1): "listed"}
+        code_tags = {("v", 1, 0): "raw_v10", ("g", 1, 0): "w_turned1"}
+        whole = {}
+
+        def cast(key, engine):
+            members = [m for m in groups if key in m][0]
+            if members not in whole:
+                whole[members] = tile("grp_%s%d%d" % key, [P, HALF * len(members), PACK], BF16, tag=cast_tags.get(key))
+            n = members.index(key)
+            interleave(nc, engine, whole[members][:, HALF * n : HALF * (n + 1), :], raw[key])
+
+        def quant(members):
+            width = HALF * len(members)
+            c = tile("cod_%s%d%d" % members[0], [P, width], U32, tag=code_tags.get(members[0]))
+            s = tile("scl_%s%d%d" % members[0], [P, width], U8)
+            nc.vector.quantize_mx(out=c[:].bitcast(FP8X4), scales=s[:], in_=whole[members][:].rearrange("p e t -> p (e t)"))
+            for n, key in enumerate(members):
+                codes[key] = c[:, HALF * n : HALF * (n + 1)]
+                scales[key] = s[:, HALF * n : HALF * (n + 1)]
+
+        q_grp = tile("q_grp", [P, Q, PACK], BF16)
+        interleave(nc, "v", q_grp[:], q_raw[:])
+        q_codes = tile("q_codes", [P, Q], U32)
+        q_scales = tile("q_scales", [P, Q], U8)
+        nc.vector.quantize_mx(out=q_codes[:].bitcast(FP8X4), scales=q_scales[:], in_=q_grp[:].rearrange("p q t -> p (q t)"))
+
+        scores = tile("scores", [P, T], F32)
+        for n in range(T // SCORE_N):
+            bank = ps.tile([P, SCORE_N], F32, name="score_ps%d" % n, tag="acc%d" % n)
+            cols = slice(SCORE_N * n, SCORE_N * (n + 1))
+            nc.tensor.matmul_mx(
+                out=bank[:],
+                lhsT=q_codes[:].bitcast(FP8X4),
+                lhsT_scale=q_scales[:],
+                rhs=k_words[:, 2 * cols.start : 2 * cols.stop].bitcast(FP4X4),
+                rhs_scale=k_scales[:, cols],
+                start=True,
+                stop=True,
+            )
+            if False:
+                nc.scalar.activation(out=scores[:, cols], in_=bank[:], func=ACT.Copy)
+            else:
+                nc.vector.tensor_copy(out=scores[:, cols], in_=bank[:])
+
+        listed = tile("listed", [P, SLOTS], F32)
+        nc.vector.tensor_copy(out=listed[:], in_=scores[:].indirect(offsets[:]))
+        neg_max = tile("neg_max", [P, 1], F32)
+        nc.vector.tensor_reduce(out=neg_max[:], in_=listed[:], axis=AXIS.X, op=ALU.max, negate=True)
+
+        p_first = tile("p_first", [P, FIRST], F32)
+        p_rest = tile("p_rest", [P, SLOTS - FIRST], F32)
+        sum_first = tile("sum_first", [P, 1], F32)
+        sum_rest = tile("sum_rest", [P, 1], F32)
+        row_sum = tile("row_sum", [P, 1], F32)
+        inv_sum = tile("inv_sum", [P, 1], F32)
+        nc.scalar.activation(out=p_first[:], in_=listed[:, 0:FIRST], func=ACT.Exp, bias=neg_max[:], accum_out=sum_first[:])
+        nc.scalar.activation(out=p_rest[:], in_=listed[:, FIRST:SLOTS], func=ACT.Exp, bias=neg_max[:], accum_out=sum_rest[:])
+        nc.scalar.activation(out=row_sum[:], in_=sum_first[:], func=ACT.Identity, bias=sum_rest[:])
+        nc.vector.tensor_copy(out=placed[:].indirect(offsets[:, 0 : FIRST // 16]), in_=p_first[:])
+        nc.vector.reciprocal(out=inv_sum[:], in_=row_sum[:])
+        nc.vector.tensor_copy(out=placed[:].indirect(offsets[:, FIRST // 16 : SLOTS // 16]), in_=p_rest[:])
+
+        fac_half = tile("fac_half", [P, PASSES, PACK], F32)
+        nc.gpsimd.tensor_scalar(out=fac_half[:], in0=fac_raw[:, :, 0:PACK], scalar1=0.5, scalar2=0.0, op0=ALU.mult, op1=ALU.add)
+        fac_rows = []
+        for g in range(PASSES):
+            bank = ps.tile([P, PACK, P], F32, name="fac_ps%d" % g, tag="fac%d" % g)
+            for j in range(PACK):
+                nc.tensor.transpose(bank[:, j, :], fac_half[:, g, j : j + 1].to_broadcast([P, P]), ident[:])
+            fac_rows.append(bank)
+
+        early = [(("g", 0, 0), "s"), (("g", 0, 1), "s"), (("v", 0, 0), "s"), (("v", 0, 1), "s"), (("g", 1, 0), "s"), (("g", 1, 1), "s"), (("v", 1, 0), "s")]
+        late = [(("v", 1, 1), "v")]
+        for key, engine in early:
+            cast(key, engine)
+
+        w_codes = []
+        w_scales = []
+        w_turned = []
+        hold = ["raw_v10", None]
+        for g in range(PASSES):
+            w_rows = tile("w_rows%d" % g, [P, K_PASS], BF16)
+            nc.vector.scalar_tensor_tensor(
+                out=w_rows[:].rearrange("q (p j) -> q p j", j=PACK),
+                in0=placed[:, K_PASS * g : K_PASS * (g + 1)].rearrange("q (p j) -> q p j", j=PACK),
+                scalar=inv_sum[:],
+                in1=fac_rows[g][:].rearrange("q j p -> q p j"),
+                op0=ALU.mult,
+                op1=ALU.mult,
+            )
+            words = w_rows[:].bitcast(F32)
+            bank = ps.tile([P, 2, Q], F32, name="turn_ps%d" % g, tag="turn%d" % g)
+            for u in range(2):
+                nc.tensor.transpose(bank[:, u, :], words[:, u : 2 * P : 2], ident[:])
+            turned = tile("w_turned%d" % g, [P, Q * PACK], BF16, tag=hold[g])
+            nc.scalar.copy(
+                out=turned[:].bitcast(F32).rearrange("p (q u) -> p q u", u=2), in_=bank[:].rearrange("p u q -> p q u")
+            )
+            w_turned.append(turned)
+        for g in range(PASSES):
+            w_codes.append(tile("w_codes%d" % g, [P, Q], U32))
+            w_scales.append(tile("w_scales%d" % g, [P, Q], U8))
+            nc.vector.quantize_mx(out=w_codes[g][:].bitcast(FP8X4), scales=w_scales[g][:], in_=w_turned[g][:])
+
+        for key, engine in late:
+            cast(key, engine)
+        for members in groups:
+            quant(members)
+
+        acc = {}
+        for n, (name, h) in enumerate([("g", 0), ("g", 1), ("v", 0), ("v", 1)]):
+            acc[name, h] = ps.tile([P, HALF], F32, name="acc_%s%d" % (name, h), tag="acc%d" % n)
+        for g in range(PASSES):
+            for name, h in acc:
+                nc.tensor.matmul_mx(
+                    out=acc[name, h][:],
+                    lhsT=w_codes[g][:].bitcast(FP8X4),
+                    lhsT_scale=w_scales[g][:],
+                    rhs=codes[name, g, h].bitcast(FP8X4),
+                    rhs_scale=scales[name, g, h],
+                    start=(g == 0),
+                    stop=(g == PASSES - 1),
+                )
+        for h in range(2):
+            gate = tile("gate%d" % h, [P, HALF], F32)
+            nc.scalar.activation(out=gate[:], in_=acc["g", h][:], func=ACT.Tanh)
+            result = tile("result%d" % h, [P, HALF], F32)
+            nc.vector.scalar_tensor_tensor(
+                out=result[:], in0=gate[:], scalar=1.0, in1=acc["v", h][:], op0=ALU.add, op1=ALU.mult
+            )
+            nc.sync.dma_start(out=out[:, HALF * h : HALF * (h + 1)], in_=result[:])

@@ -23,9 +23,10 @@ PACK = 4
 K_PASS = P * PACK
 PASSES = T // K_PASS
 HALF = E // 2
-SCORE_N = 256
 FIRST = 128
 LINE = 4
+SCORE_CUTS = [0, 512, 768, 896, 1024]
+OUT_CUTS = [0, 256, 384, 512]
 
 
 def interleave(nc, engine, grouped, raw):
@@ -74,8 +75,8 @@ def tile_attend_gatedvalues_heads_kernel(tc, query, keys_words, keys_scales, fac
                 raw[name, g, h] = t[:, :, HALF * n : HALF * (n + 1)]
 
         loads = [(n, g, [h]) for g in range(2) for n in "gv" for h in range(2)]
-        load(*loads[0])
-        load(*loads[1])
+        for item in loads[:2]:
+            load(*item)
         nc.sync.dma_start(out=fac_raw[:, :, 0:PACK], in_=fac.rearrange("o (g p j) -> p (o g) j", g=PASSES, j=PACK))
         for item in loads[2:]:
             load(*item)
@@ -87,38 +88,40 @@ def tile_attend_gatedvalues_heads_kernel(tc, query, keys_words, keys_scales, fac
 
         codes = {}
         scales = {}
+        grouped = {}
 
-        groups = [(("g", 0, 0),), (("g", 0, 1),), (("v", 0, 0),), (("v", 0, 1),), (("v", 1, 0),), (("g", 1, 0), ("g", 1, 1)), (("v", 1, 1),)]
-        cast_tags = {("v", 0, 1): "listed"}
-        code_tags = {("v", 1, 0): "raw_v10", ("g", 1, 0): "w_turned1"}
-        whole = {}
+        def cast(members, engines, tag=None):
+            grouped[members] = tile("grp_%s%d%d" % members[0], [P, HALF * len(members), PACK], BF16, tag=tag)
+            for n, key in enumerate(members):
+                interleave(nc, engines[n], grouped[members][:, HALF * n : HALF * (n + 1), :], raw[key])
 
-        def cast(key, engine):
-            members = [m for m in groups if key in m][0]
-            if members not in whole:
-                whole[members] = tile("grp_%s%d%d" % key, [P, HALF * len(members), PACK], BF16, tag=cast_tags.get(key))
-            n = members.index(key)
-            interleave(nc, engine, whole[members][:, HALF * n : HALF * (n + 1), :], raw[key])
-
-        def quant(members):
+        def quant(members, tag=None):
             width = HALF * len(members)
-            c = tile("cod_%s%d%d" % members[0], [P, width], U32, tag=code_tags.get(members[0]))
+            c = tile("cod_%s%d%d" % members[0], [P, width], U32, tag=tag)
             s = tile("scl_%s%d%d" % members[0], [P, width], U8)
-            nc.vector.quantize_mx(out=c[:].bitcast(FP8X4), scales=s[:], in_=whole[members][:].rearrange("p e t -> p (e t)"))
+            nc.vector.quantize_mx(out=c[:].bitcast(FP8X4), scales=s[:], in_=grouped[members][:].rearrange("p e t -> p (e t)"))
             for n, key in enumerate(members):
                 codes[key] = c[:, HALF * n : HALF * (n + 1)]
                 scales[key] = s[:, HALF * n : HALF * (n + 1)]
 
+        g0a, g0b, v0a, v0b = (("g", 0, 0),), (("g", 0, 1),), (("v", 0, 0),), (("v", 0, 1),)
+        g1, v1a, v1b = (("g", 1, 0), ("g", 1, 1)), (("v", 1, 0),), (("v", 1, 1),)
+
         q_grp = tile("q_grp", [P, Q, PACK], BF16)
-        interleave(nc, "v", q_grp[:], q_raw[:])
         q_codes = tile("q_codes", [P, Q], U32)
         q_scales = tile("q_scales", [P, Q], U8)
-        nc.vector.quantize_mx(out=q_codes[:].bitcast(FP8X4), scales=q_scales[:], in_=q_grp[:].rearrange("p q t -> p (q t)"))
+        q_halves = [slice(0, Q // 2), slice(Q // 2, Q)]
+        for cols in q_halves:
+            interleave(nc, "v", q_grp[:, cols, :], q_raw[:, :, cols])
+        for cols in q_halves:
+            nc.vector.quantize_mx(
+                out=q_codes[:, cols].bitcast(FP8X4), scales=q_scales[:, cols], in_=q_grp[:, cols, :].rearrange("p q t -> p (q t)")
+            )
 
         scores = tile("scores", [P, T], F32)
-        for n in range(T // SCORE_N):
-            bank = ps.tile([P, SCORE_N], F32, name="score_ps%d" % n, tag="acc%d" % n)
-            cols = slice(SCORE_N * n, SCORE_N * (n + 1))
+        for n in range(len(SCORE_CUTS) - 1):
+            cols = slice(SCORE_CUTS[n], SCORE_CUTS[n + 1])
+            bank = ps.tile([P, cols.stop - cols.start], F32, name="score_ps%d" % n, tag="bank%d" % n)
             nc.tensor.matmul_mx(
                 out=bank[:],
                 lhsT=q_codes[:].bitcast(FP8X4),
@@ -128,61 +131,60 @@ def tile_attend_gatedvalues_heads_kernel(tc, query, keys_words, keys_scales, fac
                 start=True,
                 stop=True,
             )
-            if False:
-                nc.scalar.activation(out=scores[:, cols], in_=bank[:], func=ACT.Copy)
-            else:
-                nc.vector.tensor_copy(out=scores[:, cols], in_=bank[:])
+            nc.vector.tensor_copy(out=scores[:, cols], in_=bank[:])
 
         listed = tile("listed", [P, SLOTS], F32)
         nc.vector.tensor_copy(out=listed[:], in_=scores[:].indirect(offsets[:]))
         neg_max = tile("neg_max", [P, 1], F32)
         nc.vector.tensor_reduce(out=neg_max[:], in_=listed[:], axis=AXIS.X, op=ALU.max, negate=True)
 
-        p_first = tile("p_first", [P, FIRST], F32)
-        p_rest = tile("p_rest", [P, SLOTS - FIRST], F32)
-        sum_first = tile("sum_first", [P, 1], F32)
-        sum_rest = tile("sum_rest", [P, 1], F32)
+        for members in (g0a, g0b, v0a):
+            cast(members, "s")
+        p_first = tile("p_first", [P, FIRST], F32, tag="raw_v00")
+        p_all = tile("p_all", [P, SLOTS], F32)
         row_sum = tile("row_sum", [P, 1], F32)
         inv_sum = tile("inv_sum", [P, 1], F32)
-        nc.scalar.activation(out=p_first[:], in_=listed[:, 0:FIRST], func=ACT.Exp, bias=neg_max[:], accum_out=sum_first[:])
-        nc.scalar.activation(out=p_rest[:], in_=listed[:, FIRST:SLOTS], func=ACT.Exp, bias=neg_max[:], accum_out=sum_rest[:])
-        nc.scalar.activation(out=row_sum[:], in_=sum_first[:], func=ACT.Identity, bias=sum_rest[:])
+        nc.scalar.activation(out=p_first[:], in_=listed[:, 0:FIRST], func=ACT.Exp, bias=neg_max[:])
+        nc.scalar.activation(out=p_all[:], in_=listed[:], func=ACT.Exp, bias=neg_max[:], accum_out=row_sum[:])
         nc.vector.tensor_copy(out=placed[:].indirect(offsets[:, 0 : FIRST // 16]), in_=p_first[:])
         nc.vector.reciprocal(out=inv_sum[:], in_=row_sum[:])
-        nc.vector.tensor_copy(out=placed[:].indirect(offsets[:, FIRST // 16 : SLOTS // 16]), in_=p_rest[:])
+        nc.vector.tensor_copy(out=placed[:].indirect(offsets[:, FIRST // 16 : SLOTS // 16]), in_=p_all[:, FIRST:SLOTS])
 
         fac_half = tile("fac_half", [P, PASSES, PACK], F32)
         nc.gpsimd.tensor_scalar(out=fac_half[:], in0=fac_raw[:, :, 0:PACK], scalar1=0.5, scalar2=0.0, op0=ALU.mult, op1=ALU.add)
         fac_rows = []
         for g in range(PASSES):
-            bank = ps.tile([P, PACK, P], F32, name="fac_ps%d" % g, tag="fac%d" % g)
+            bank = ps.tile([P, PACK, P], F32, name="fac_ps%d" % g, tag="bank%d" % (4 + g))
             for j in range(PACK):
                 nc.tensor.transpose(bank[:, j, :], fac_half[:, g, j : j + 1].to_broadcast([P, P]), ident[:])
             fac_rows.append(bank)
 
-        early = [(("g", 0, 0), "s"), (("g", 0, 1), "s"), (("v", 0, 0), "s"), (("v", 0, 1), "s"), (("g", 1, 0), "s"), (("g", 1, 1), "s"), (("v", 1, 0), "s")]
-        late = [(("v", 1, 1), "v")]
-        for key, engine in early:
-            cast(key, engine)
+        cast(v0b, "s", tag="listed")
+        cast(g1, "ss")
+        cast(v1a, "s")
 
+        quant(v0b)
+        for members in (g0a, g0b, v0a, g1, v1a):
+            quant(members)
         w_codes = []
         w_scales = []
         w_turned = []
-        hold = ["raw_v10", None]
+        hold = ["raw_v10", "grp_v10"]
+        w_all = tile("w_all", [P, PASSES, 2, 2 * P], BF16, tag="raw_v01")
         for g in range(PASSES):
-            w_rows = tile("w_rows%d" % g, [P, K_PASS], BF16)
-            nc.vector.scalar_tensor_tensor(
-                out=w_rows[:].rearrange("q (p j) -> q p j", j=PACK),
-                in0=placed[:, K_PASS * g : K_PASS * (g + 1)].rearrange("q (p j) -> q p j", j=PACK),
-                scalar=inv_sum[:],
-                in1=fac_rows[g][:].rearrange("q j p -> q p j"),
-                op0=ALU.mult,
-                op1=ALU.mult,
-            )
-            words = w_rows[:].bitcast(F32)
-            bank = ps.tile([P, 2, Q], F32, name="turn_ps%d" % g, tag="turn%d" % g)
+            bank = ps.tile([P, 2, Q], F32, name="turn_ps%d" % g, tag="bank%d" % (6 + g))
             for u in range(2):
-                nc.tensor.transpose(bank[:, u, :], words[:, u : 2 * P : 2], ident[:])
+                pair = slice(2 * u, 2 * u + 2)
+                w_rows = w_all[:, g, u, :]
+                nc.vector.scalar_tensor_tensor(
+                    out=w_rows.rearrange("q (p j) -> q p j", j=2),
+                    in0=placed[:, K_PASS * g : K_PASS * (g + 1)].rearrange("q (p j) -> q p j", j=PACK)[:, :, pair],
+                    scalar=inv_sum[:],
+                    in1=fac_rows[g][:, pair, :].rearrange("q j p -> q p j"),
+                    op0=ALU.mult,
+                    op1=ALU.mult,
+                )
+                nc.tensor.transpose(bank[:, u, :], w_rows.bitcast(F32), ident[:])
             turned = tile("w_turned%d" % g, [P, Q * PACK], BF16, tag=hold[g])
             nc.scalar.copy(
                 out=turned[:].bitcast(F32).rearrange("p (q u) -> p q u", u=2), in_=bank[:].rearrange("p u q -> p q u")
@@ -192,31 +194,33 @@ def tile_attend_gatedvalues_heads_kernel(tc, query, keys_words, keys_scales, fac
             w_codes.append(tile("w_codes%d" % g, [P, Q], U32))
             w_scales.append(tile("w_scales%d" % g, [P, Q], U8))
             nc.vector.quantize_mx(out=w_codes[g][:].bitcast(FP8X4), scales=w_scales[g][:], in_=w_turned[g][:])
+        cast(v1b, "v", tag="raw_v10")
+        quant(v1b)
 
-        for key, engine in late:
-            cast(key, engine)
-        for members in groups:
-            quant(members)
-
+        pieces = [("g", 0, HALF), ("g", HALF, E)] + [("v", OUT_CUTS[n], OUT_CUTS[n + 1]) for n in range(len(OUT_CUTS) - 1)]
         acc = {}
-        for n, (name, h) in enumerate([("g", 0), ("g", 1), ("v", 0), ("v", 1)]):
-            acc[name, h] = ps.tile([P, HALF], F32, name="acc_%s%d" % (name, h), tag="acc%d" % n)
-        for g in range(PASSES):
-            for name, h in acc:
+        for n, (name, lo, hi) in enumerate(pieces):
+            acc[name, lo, hi] = ps.tile([P, hi - lo], F32, name="acc_%s%d" % (name, lo), tag="bank%d" % n)
+        passes = [(0, x) for x in pieces[:3]] + [(1, x) for x in pieces[:2]] + [(0, x) for x in pieces[3:]] + [(1, x) for x in pieces[2:]]
+        if True:
+            for g, (name, lo, hi) in passes:
+                within = slice(lo % HALF, lo % HALF + hi - lo)
                 nc.tensor.matmul_mx(
-                    out=acc[name, h][:],
+                    out=acc[name, lo, hi][:],
                     lhsT=w_codes[g][:].bitcast(FP8X4),
                     lhsT_scale=w_scales[g][:],
-                    rhs=codes[name, g, h].bitcast(FP8X4),
-                    rhs_scale=scales[name, g, h],
+                    rhs=codes[name, g, lo // HALF][:, within].bitcast(FP8X4),
+                    rhs_scale=scales[name, g, lo // HALF][:, within],
                     start=(g == 0),
                     stop=(g == PASSES - 1),
                 )
-        for h in range(2):
-            gate = tile("gate%d" % h, [P, HALF], F32)
-            nc.scalar.activation(out=gate[:], in_=acc["g", h][:], func=ACT.Tanh)
-            result = tile("result%d" % h, [P, HALF], F32)
-            nc.vector.scalar_tensor_tensor(
-                out=result[:], in0=gate[:], scalar=1.0, in1=acc["v", h][:], op0=ALU.add, op1=ALU.mult
-            )
-            nc.sync.dma_start(out=out[:, HALF * h : HALF * (h + 1)], in_=result[:])
+        gate = tile("gate", [P, E], F32)
+        for name, lo, hi in pieces:
+            if name == "g":
+                nc.scalar.activation(out=gate[:, lo:hi], in_=acc[name, lo, hi][:], func=ACT.Tanh)
+            else:
+                result = tile("result%d" % lo, [P, hi - lo], F32)
+                nc.vector.scalar_tensor_tensor(
+                    out=result[:], in0=gate[:, lo:hi], scalar=1.0, in1=acc[name, lo, hi][:], op0=ALU.add, op1=ALU.mult
+                )
+                nc.sync.dma_start(out=out[:, lo:hi], in_=result[:])

@@ -22,34 +22,60 @@ P = 128
 PACK = 4
 K_PASS = P * PACK
 PASSES = T // K_PASS
-HALF = E // 2
-FIRST = 128
+PER_COLUMN = 16
 LINE = 4
-SCORE_CUTS = [0, 512, 768, 896, 1024]
-OUT_CUTS = [0, 256, 384, 512]
+HALF = E // 2
+QUARTER = E // 4
+FIRST = 128
+SCORE_COLS = (slice(0, 512), slice(512, 768), slice(768, 896), slice(896, 1024))
+GATE_COLS = (slice(0, HALF), slice(HALF, E))
+OUT_COLS = (slice(0, HALF), slice(HALF, HALF + QUARTER), slice(HALF + QUARTER, E))
 
 
-def interleave(nc, engine, grouped, raw):
-    dst = grouped.rearrange("p (c i) t -> p c t i", i=LINE)
-    src = raw.rearrange("p t (c i) -> p c t i", i=LINE)
-    if engine == "v":
-        nc.vector.tensor_copy(out=dst, in_=src)
-    elif engine == "s":
-        nc.scalar.activation(out=dst, in_=src, func=ACT.Copy)
-    else:
-        nc.gpsimd.tensor_scalar(out=dst, in0=src, scalar1=1.0, scalar2=0.0, op0=ALU.mult, op1=ALU.add)
+def interleave_views(grouped, raw):
+    return (
+        grouped.rearrange("p (c i) j -> p c j i", i=LINE),
+        raw.rearrange("p j (c i) -> p c j i", i=LINE),
+    )
+
+
+def interleave_on_vector(nc, grouped, raw):
+    dst, src = interleave_views(grouped, raw)
+    nc.vector.tensor_copy(out=dst, in_=src)
+
+
+def interleave_on_scalar(nc, grouped, raw):
+    dst, src = interleave_views(grouped, raw)
+    nc.scalar.activation(out=dst, in_=src, func=ACT.Copy)
 
 
 def tile_attend_gatedvalues_heads_kernel(tc, query, keys_words, keys_scales, fac, vals, gval, offs, out):
     nc = tc.nc
     with ExitStack() as ctx:
-        sb = ctx.enter_context(tc.tile_pool(name="sb", bufs=1))
-        ps = ctx.enter_context(tc.psum_pool(name="ps", bufs=1))
+        sbuf = ctx.enter_context(tc.tile_pool(name="sbuf", bufs=1))
+        psum = ctx.enter_context(tc.psum_pool(name="psum", bufs=1))
 
         def tile(name, shape, dtype, tag=None):
-            return sb.tile(shape, dtype, name=name, tag=tag or name, align_bytes=64)
+            return sbuf.tile(shape, dtype, name=name, tag=tag or name, align_bytes=64)
 
-        offsets = sb.tile([P, SLOTS // 16], U16, name="offsets")
+        def bank(name, shape, number):
+            return psum.tile(shape, F32, name=name, tag="bank%d" % number)
+
+        def load_pass(name, source, g, cols):
+            raw = tile(name, [P, PACK, cols.stop - cols.start], F32)
+            rows = source[K_PASS * g : K_PASS * (g + 1), :].rearrange("(p j) e -> p j e", j=PACK)
+            nc.sync.dma_start(out=raw[:], in_=rows[:, :, cols])
+            return raw
+
+        def quantise(name, grouped):
+            words = tile(name + "_words", [P, grouped.shape[1]], U32)
+            scale_bytes = tile(name + "_scales", [P, grouped.shape[1]], U8)
+            nc.vector.quantize_mx(
+                out=words[:].bitcast(FP8X4), scales=scale_bytes[:], in_=grouped.rearrange("p x j -> p (x j)")
+            )
+            return words, scale_bytes
+
+        offsets = sbuf.tile([P, SLOTS // PER_COLUMN], U16, name="offsets")
         q_raw = tile("q_raw", [P, PACK, Q], F32)
         k_words = tile("k_words", [P, 2 * T], U8)
         k_scales = tile("k_scales", [P, T], U8)
@@ -63,164 +89,155 @@ def tile_attend_gatedvalues_heads_kernel(tc, query, keys_words, keys_scales, fac
                 in_=keys_scales[0, 4 * quad : 4 * quad + 4, :].bitcast(I32),
             )
         nc.sync.dma_start(offsets[:], offs)
-
-        sources = {"g": gval, "v": vals}
-        raw = {}
-
-        def load(name, g, halves):
-            rows = sources[name][K_PASS * g : K_PASS * (g + 1), :].rearrange("(p j) e -> p j e", j=PACK)
-            t = tile("raw_%s%d%d" % (name, g, halves[0]), [P, PACK, HALF * len(halves)], F32)
-            nc.sync.dma_start(out=t[:], in_=rows[:, :, HALF * halves[0] : HALF * (halves[-1] + 1)])
-            for n, h in enumerate(halves):
-                raw[name, g, h] = t[:, :, HALF * n : HALF * (n + 1)]
-
-        loads = [(n, g, [h]) for g in range(2) for n in "gv" for h in range(2)]
-        for item in loads[:2]:
-            load(*item)
+        g0_raw = [load_pass("g0_raw%d" % h, gval, 0, GATE_COLS[h]) for h in range(2)]
         nc.sync.dma_start(out=fac_raw[:, :, 0:PACK], in_=fac.rearrange("o (g p j) -> p (o g) j", g=PASSES, j=PACK))
-        for item in loads[2:]:
-            load(*item)
+        v0_raw = load_pass("v0_raw", vals, 0, slice(0, E))
+        g1_raw = load_pass("g1_raw", gval, 1, slice(0, E))
+        v1_raw = load_pass("v1_raw", vals, 1, slice(0, E))
 
         ident = tile("ident", [P, P], F32)
-        make_identity(nc, ident[:])
+        nc.vector.memset(ident[:], 0.0)
+        make_identity(nc, ident[:], nomemset=True)
         placed = tile("placed", [P, T], F32)
-        nc.gpsimd.memset(placed[:], 0.0)
+        nc.vector.memset(placed[:], 0.0)
 
-        codes = {}
-        scales = {}
-        grouped = {}
-
-        def cast(members, engines, tag=None):
-            grouped[members] = tile("grp_%s%d%d" % members[0], [P, HALF * len(members), PACK], BF16, tag=tag)
-            for n, key in enumerate(members):
-                interleave(nc, engines[n], grouped[members][:, HALF * n : HALF * (n + 1), :], raw[key])
-
-        def quant(members, tag=None):
-            width = HALF * len(members)
-            c = tile("cod_%s%d%d" % members[0], [P, width], U32, tag=tag)
-            s = tile("scl_%s%d%d" % members[0], [P, width], U8)
-            nc.vector.quantize_mx(out=c[:].bitcast(FP8X4), scales=s[:], in_=grouped[members][:].rearrange("p e t -> p (e t)"))
-            for n, key in enumerate(members):
-                codes[key] = c[:, HALF * n : HALF * (n + 1)]
-                scales[key] = s[:, HALF * n : HALF * (n + 1)]
-
-        g0a, g0b, v0a, v0b = (("g", 0, 0),), (("g", 0, 1),), (("v", 0, 0),), (("v", 0, 1),)
-        g1, v1a, v1b = (("g", 1, 0), ("g", 1, 1)), (("v", 1, 0),), (("v", 1, 1),)
-
-        q_grp = tile("q_grp", [P, Q, PACK], BF16)
-        q_codes = tile("q_codes", [P, Q], U32)
+        q_grouped = tile("q_grouped", [P, Q, PACK], BF16)
+        q_words = tile("q_words", [P, Q], U32)
         q_scales = tile("q_scales", [P, Q], U8)
-        q_halves = [slice(0, Q // 2), slice(Q // 2, Q)]
+        q_halves = (slice(0, Q // 2), slice(Q // 2, Q))
         for cols in q_halves:
-            interleave(nc, "v", q_grp[:, cols, :], q_raw[:, :, cols])
+            interleave_on_vector(nc, q_grouped[:, cols, :], q_raw[:, :, cols])
         for cols in q_halves:
             nc.vector.quantize_mx(
-                out=q_codes[:, cols].bitcast(FP8X4), scales=q_scales[:, cols], in_=q_grp[:, cols, :].rearrange("p q t -> p (q t)")
+                out=q_words[:, cols].bitcast(FP8X4),
+                scales=q_scales[:, cols],
+                in_=q_grouped[:, cols, :].rearrange("p q j -> p (q j)"),
             )
-
         scores = tile("scores", [P, T], F32)
-        for n in range(len(SCORE_CUTS) - 1):
-            cols = slice(SCORE_CUTS[n], SCORE_CUTS[n + 1])
-            bank = ps.tile([P, cols.stop - cols.start], F32, name="score_ps%d" % n, tag="bank%d" % n)
+        for n, cols in enumerate(SCORE_COLS):
+            score_sums = bank("score_sums%d" % n, [P, cols.stop - cols.start], n)
             nc.tensor.matmul_mx(
-                out=bank[:],
-                lhsT=q_codes[:].bitcast(FP8X4),
+                out=score_sums[:],
+                lhsT=q_words[:].bitcast(FP8X4),
                 lhsT_scale=q_scales[:],
                 rhs=k_words[:, 2 * cols.start : 2 * cols.stop].bitcast(FP4X4),
                 rhs_scale=k_scales[:, cols],
                 start=True,
                 stop=True,
             )
-            nc.vector.tensor_copy(out=scores[:, cols], in_=bank[:])
+            if n == 0:
+                nc.scalar.activation(out=scores[:, cols], in_=score_sums[:], func=ACT.Copy)
+            else:
+                nc.vector.tensor_copy(out=scores[:, cols], in_=score_sums[:])
 
         listed = tile("listed", [P, SLOTS], F32)
         nc.vector.tensor_copy(out=listed[:], in_=scores[:].indirect(offsets[:]))
         neg_max = tile("neg_max", [P, 1], F32)
         nc.vector.tensor_reduce(out=neg_max[:], in_=listed[:], axis=AXIS.X, op=ALU.max, negate=True)
 
-        for members in (g0a, g0b, v0a):
-            cast(members, "s")
-        p_first = tile("p_first", [P, FIRST], F32, tag="raw_v00")
+        g0_grouped = tile("g0_grouped", [P, E, PACK], BF16, tag="k_words")
+        for h, cols in enumerate(GATE_COLS):
+            interleave_on_scalar(nc, g0_grouped[:, cols, :], g0_raw[h][:])
+
+        p_first = tile("p_first", [P, FIRST], F32, tag="g0_raw1")
         p_all = tile("p_all", [P, SLOTS], F32)
         row_sum = tile("row_sum", [P, 1], F32)
         inv_sum = tile("inv_sum", [P, 1], F32)
+        cut = FIRST // PER_COLUMN
         nc.scalar.activation(out=p_first[:], in_=listed[:, 0:FIRST], func=ACT.Exp, bias=neg_max[:])
         nc.scalar.activation(out=p_all[:], in_=listed[:], func=ACT.Exp, bias=neg_max[:], accum_out=row_sum[:])
-        nc.vector.tensor_copy(out=placed[:].indirect(offsets[:, 0 : FIRST // 16]), in_=p_first[:])
+        nc.vector.tensor_copy(out=placed[:].indirect(offsets[:, 0:cut]), in_=p_first[:])
         nc.vector.reciprocal(out=inv_sum[:], in_=row_sum[:])
-        nc.vector.tensor_copy(out=placed[:].indirect(offsets[:, FIRST // 16 : SLOTS // 16]), in_=p_all[:, FIRST:SLOTS])
+        nc.vector.tensor_copy(out=placed[:].indirect(offsets[:, cut : SLOTS // PER_COLUMN]), in_=p_all[:, FIRST:SLOTS])
 
         fac_half = tile("fac_half", [P, PASSES, PACK], F32)
-        nc.gpsimd.tensor_scalar(out=fac_half[:], in0=fac_raw[:, :, 0:PACK], scalar1=0.5, scalar2=0.0, op0=ALU.mult, op1=ALU.add)
+        nc.gpsimd.tensor_scalar(
+            out=fac_half[:], in0=fac_raw[:, :, 0:PACK], scalar1=0.5, scalar2=0.0, op0=ALU.mult, op1=ALU.add
+        )
         fac_rows = []
         for g in range(PASSES):
-            bank = ps.tile([P, PACK, P], F32, name="fac_ps%d" % g, tag="bank%d" % (4 + g))
+            rows = bank("fac_rows%d" % g, [P, PACK, P], 4 + g)
             for j in range(PACK):
-                nc.tensor.transpose(bank[:, j, :], fac_half[:, g, j : j + 1].to_broadcast([P, P]), ident[:])
-            fac_rows.append(bank)
+                nc.tensor.transpose(rows[:, j, :], fac_half[:, g, j : j + 1].to_broadcast([P, P]), ident[:])
+            fac_rows.append(rows)
 
-        cast(v0b, "s", tag="listed")
-        cast(g1, "ss")
-        cast(v1a, "s")
+        v0_grouped = tile("v0_grouped", [P, E, PACK], BF16, tag="listed")
+        g1_grouped = tile("g1_grouped", [P, E, PACK], BF16)
+        for grouped, raw in ((v0_grouped, v0_raw), (g1_grouped, g1_raw)):
+            for cols in GATE_COLS:
+                interleave_on_scalar(nc, grouped[:, cols, :], raw[:, :, cols])
+        g0 = quantise("g0", g0_grouped[:])
+        v0 = quantise("v0", v0_grouped[:])
+        g1 = quantise("g1", g1_grouped[:])
 
-        quant(v0b)
-        for members in (g0a, g0b, v0a, g1, v1a):
-            quant(members)
-        w_codes = []
-        w_scales = []
+        w_pairs = tile("w_pairs", [P, PASSES, 2, 2 * P], BF16, tag="v0_raw")
         w_turned = []
-        hold = ["raw_v10", "grp_v10"]
-        w_all = tile("w_all", [P, PASSES, 2, 2 * P], BF16, tag="raw_v01")
-        for g in range(PASSES):
-            bank = ps.tile([P, 2, Q], F32, name="turn_ps%d" % g, tag="bank%d" % (6 + g))
+        for g, reused in enumerate(("g1_raw", "g1_grouped")):
+            turned_words = bank("turned_words%d" % g, [P, 2, Q], 6 + g)
             for u in range(2):
                 pair = slice(2 * u, 2 * u + 2)
-                w_rows = w_all[:, g, u, :]
                 nc.vector.scalar_tensor_tensor(
-                    out=w_rows.rearrange("q (p j) -> q p j", j=2),
+                    out=w_pairs[:, g, u, :].rearrange("q (p j) -> q p j", j=2),
                     in0=placed[:, K_PASS * g : K_PASS * (g + 1)].rearrange("q (p j) -> q p j", j=PACK)[:, :, pair],
                     scalar=inv_sum[:],
                     in1=fac_rows[g][:, pair, :].rearrange("q j p -> q p j"),
                     op0=ALU.mult,
                     op1=ALU.mult,
                 )
-                nc.tensor.transpose(bank[:, u, :], w_rows.bitcast(F32), ident[:])
-            turned = tile("w_turned%d" % g, [P, Q * PACK], BF16, tag=hold[g])
+                nc.tensor.transpose(turned_words[:, u, :], w_pairs[:, g, u, :].bitcast(F32), ident[:])
+            turned = tile("w_turned%d" % g, [P, Q * PACK], BF16, tag=reused)
             nc.scalar.copy(
-                out=turned[:].bitcast(F32).rearrange("p (q u) -> p q u", u=2), in_=bank[:].rearrange("p u q -> p q u")
+                out=turned[:].bitcast(F32).rearrange("p (q u) -> p q u", u=2),
+                in_=turned_words[:].rearrange("p u q -> p q u"),
             )
             w_turned.append(turned)
-        for g in range(PASSES):
-            w_codes.append(tile("w_codes%d" % g, [P, Q], U32))
-            w_scales.append(tile("w_scales%d" % g, [P, Q], U8))
-            nc.vector.quantize_mx(out=w_codes[g][:].bitcast(FP8X4), scales=w_scales[g][:], in_=w_turned[g][:])
-        cast(v1b, "v", tag="raw_v10")
-        quant(v1b)
+        weights = [
+            quantise("w%d" % g, w_turned[g][:].rearrange("p (q j) -> p q j", j=PACK)) for g in range(PASSES)
+        ]
 
-        pieces = [("g", 0, HALF), ("g", HALF, E)] + [("v", OUT_CUTS[n], OUT_CUTS[n + 1]) for n in range(len(OUT_CUTS) - 1)]
-        acc = {}
-        for n, (name, lo, hi) in enumerate(pieces):
-            acc[name, lo, hi] = ps.tile([P, hi - lo], F32, name="acc_%s%d" % (name, lo), tag="bank%d" % n)
-        passes = [(0, x) for x in pieces[:3]] + [(1, x) for x in pieces[:2]] + [(0, x) for x in pieces[3:]] + [(1, x) for x in pieces[2:]]
-        if True:
-            for g, (name, lo, hi) in passes:
-                within = slice(lo % HALF, lo % HALF + hi - lo)
-                nc.tensor.matmul_mx(
-                    out=acc[name, lo, hi][:],
-                    lhsT=w_codes[g][:].bitcast(FP8X4),
-                    lhsT_scale=w_scales[g][:],
-                    rhs=codes[name, g, lo // HALF][:, within].bitcast(FP8X4),
-                    rhs_scale=scales[name, g, lo // HALF][:, within],
-                    start=(g == 0),
-                    stop=(g == PASSES - 1),
-                )
+        v1_grouped = tile("v1_grouped", [P, E, PACK], BF16, tag="g1_raw")
+        for cols in OUT_COLS[:2]:
+            interleave_on_vector(nc, v1_grouped[:, cols, :], v1_raw[:, :, cols])
+        interleave_on_scalar(nc, v1_grouped[:, OUT_COLS[2], :], v1_raw[:, :, OUT_COLS[2]])
+        v1_halves = [quantise("v1_%d" % h, v1_grouped[:, cols, :]) for h, cols in enumerate(GATE_COLS)]
+
+        def gate_operand(g, cols):
+            words, scale_bytes = (g0, g1)[g]
+            return words[:, cols], scale_bytes[:, cols]
+
+        def value_operand(g, cols):
+            if g == 0:
+                return v0[0][:, cols], v0[1][:, cols]
+            words, scale_bytes = v1_halves[cols.start // HALF]
+            inside = slice(cols.start % HALF, cols.start % HALF + cols.stop - cols.start)
+            return words[:, inside], scale_bytes[:, inside]
+
+        gate_sums = [bank("gate_sums%d" % n, [P, HALF], n) for n in range(len(GATE_COLS))]
+        value_sums = [
+            bank("value_sums%d" % n, [P, cols.stop - cols.start], len(GATE_COLS) + n) for n, cols in enumerate(OUT_COLS)
+        ]
+        products = [(gate_sums[n], gate_operand, cols) for n, cols in enumerate(GATE_COLS)]
+        products.extend((value_sums[n], value_operand, cols) for n, cols in enumerate(OUT_COLS))
+        for run in (products[:3], products[3:]):
+            for g in range(PASSES):
+                for sums, operand, cols in run:
+                    words, scale_bytes = operand(g, cols)
+                    nc.tensor.matmul_mx(
+                        out=sums[:],
+                        lhsT=weights[g][0][:].bitcast(FP8X4),
+                        lhsT_scale=weights[g][1][:],
+                        rhs=words.bitcast(FP8X4),
+                        rhs_scale=scale_bytes,
+                        start=(g == 0),
+                        stop=(g == PASSES - 1),
+                    )
+
         gate = tile("gate", [P, E], F32)
-        for name, lo, hi in pieces:
-            if name == "g":
-                nc.scalar.activation(out=gate[:, lo:hi], in_=acc[name, lo, hi][:], func=ACT.Tanh)
-            else:
-                result = tile("result%d" % lo, [P, hi - lo], F32)
-                nc.vector.scalar_tensor_tensor(
-                    out=result[:], in0=gate[:, lo:hi], scalar=1.0, in1=acc[name, lo, hi][:], op0=ALU.add, op1=ALU.mult
-                )
-                nc.sync.dma_start(out=out[:, lo:hi], in_=result[:])
+        for n, cols in enumerate(GATE_COLS):
+            nc.scalar.activation(out=gate[:, cols], in_=gate_sums[n][:], func=ACT.Tanh)
+        for n, cols in enumerate(OUT_COLS):
+            result = tile("result%d" % n, [P, cols.stop - cols.start], F32)
+            nc.vector.scalar_tensor_tensor(
+                out=result[:], in0=gate[:, cols], scalar=1.0, in1=value_sums[n][:], op0=ALU.add, op1=ALU.mult
+            )
+            nc.sync.dma_start(out=out[:, cols], in_=result[:])

@@ -218,6 +218,17 @@ def tile_attend_gatedvalues_heads_kernel(tc, query, keys_words, keys_scales, fac
         ]
         products = [(gate_sums[n], gate_operand, cols) for n, cols in enumerate(GATE_COLS)]
         products.extend((value_sums[n], value_operand, cols) for n, cols in enumerate(OUT_COLS))
+        unused_sums = bank("unused_sums", [P, E], 4 + PASSES - 1)
+        for width in (E, QUARTER):
+            nc.tensor.matmul_mx(
+                out=unused_sums[:, 0:width],
+                lhsT=q_words[:].bitcast(FP8X4),
+                lhsT_scale=q_scales[:],
+                rhs=v0[0][:, 0:width].bitcast(FP8X4),
+                rhs_scale=v0[1][:, 0:width],
+                start=True,
+                stop=True,
+            )
         for run in (products[:3], products[3:]):
             for g in range(PASSES):
                 for sums, operand, cols in run:

@@ -1,3 +1,4 @@
+import itertools
 from contextlib import ExitStack
 
 import concourse.mybir as mybir
@@ -27,7 +28,7 @@ LINE = 4
 HALF = E // 2
 QUARTER = E // 4
 FIRST = 128
-SCORE_COLS = (slice(0, 512), slice(512, 768), slice(768, 896), slice(896, 1024))
+SCORE_COLS = (slice(0, 256), slice(256, 512), slice(512, 768), slice(768, 1024))
 GATE_COLS = (slice(0, HALF), slice(HALF, E))
 OUT_COLS = (slice(0, HALF), slice(HALF, HALF + QUARTER), slice(HALF + QUARTER, E))
 
@@ -49,26 +50,42 @@ def interleave_on_scalar(nc, grouped, raw):
     nc.scalar.activation(out=dst, in_=src, func=ACT.Copy)
 
 
+def interleave_on_gpsimd(nc, grouped, raw):
+    nc.gpsimd.tensor_scalar(out=grouped, in0=raw.rearrange("p j x -> p x j"), scalar1=1.0, scalar2=0.0, op0=ALU.mult, op1=ALU.add)
+
+
 def tile_attend_gatedvalues_heads_kernel(tc, query, keys_words, keys_scales, fac, vals, gval, offs, out):
     nc = tc.nc
     with ExitStack() as ctx:
         sbuf = ctx.enter_context(tc.tile_pool(name="sbuf", bufs=1))
+        shared = ctx.enter_context(tc.tile_pool(name="shared", bufs=1))
         psum = ctx.enter_context(tc.psum_pool(name="psum", bufs=1))
 
-        def tile(name, shape, dtype, tag=None):
+        def tile(name, shape, dtype, tag=None, offset=None):
+            if offset is not None:
+                return shared.tile(shape, dtype, name=name, align_bytes=64, offset=offset)
             return sbuf.tile(shape, dtype, name=name, tag=tag or name, align_bytes=64)
 
         def bank(name, shape, number):
             return psum.tile(shape, F32, name=name, tag="bank%d" % number)
 
-        def load_pass(name, source, g, cols):
-            raw = tile(name, [P, PACK, cols.stop - cols.start], F32)
+        def load_pass(name, source, g, cols, offset=None):
+            raw = tile(name, [P, PACK, cols.stop - cols.start], F32, offset=offset)
             rows = source[K_PASS * g : K_PASS * (g + 1), :].rearrange("(p j) e -> p j e", j=PACK)
             nc.sync.dma_start(out=raw[:], in_=rows[:, :, cols])
             return raw
 
-        def quantise(name, grouped):
-            words = tile(name + "_words", [P, grouped.shape[1]], U32)
+        def load_pairs(name, source, g):
+            rows = source[K_PASS * g : K_PASS * (g + 1), :].rearrange("(p u j) e -> p u j e", u=2, j=2)
+            pairs = []
+            for u in range(2):
+                raw = tile("%s%d" % (name, u), [P, 2, E], F32)
+                nc.sync.dma_start(out=raw[:], in_=rows[:, u, :, :])
+                pairs.append(raw)
+            return pairs
+
+        def quantise(name, grouped, tag=None, offset=None):
+            words = tile(name + "_words", [P, grouped.shape[1]], U32, tag=tag, offset=offset)
             scale_bytes = tile(name + "_scales", [P, grouped.shape[1]], U8)
             nc.vector.quantize_mx(
                 out=words[:].bitcast(FP8X4), scales=scale_bytes[:], in_=grouped.rearrange("p x j -> p (x j)")
@@ -89,10 +106,10 @@ def tile_attend_gatedvalues_heads_kernel(tc, query, keys_words, keys_scales, fac
                 in_=keys_scales[0, 4 * quad : 4 * quad + 4, :].bitcast(I32),
             )
         nc.sync.dma_start(offsets[:], offs)
-        g0_raw = [load_pass("g0_raw%d" % h, gval, 0, GATE_COLS[h]) for h in range(2)]
+        g0_raw = load_pairs("g0_raw", gval, 0)
         nc.sync.dma_start(out=fac_raw[:, :, 0:PACK], in_=fac.rearrange("o (g p j) -> p (o g) j", g=PASSES, j=PACK))
         v0_raw = load_pass("v0_raw", vals, 0, slice(0, E))
-        g1_raw = load_pass("g1_raw", gval, 1, slice(0, E))
+        g1_raw = load_pass("g1_raw", gval, 1, slice(0, E), offset=0)
         v1_raw = load_pass("v1_raw", vals, 1, slice(0, E))
 
         ident = tile("ident", [P, P], F32)
@@ -105,14 +122,11 @@ def tile_attend_gatedvalues_heads_kernel(tc, query, keys_words, keys_scales, fac
         q_words = tile("q_words", [P, Q], U32)
         q_scales = tile("q_scales", [P, Q], U8)
         q_halves = (slice(0, Q // 2), slice(Q // 2, Q))
-        for cols in q_halves:
-            interleave_on_vector(nc, q_grouped[:, cols, :], q_raw[:, :, cols])
-        for cols in q_halves:
-            nc.vector.quantize_mx(
-                out=q_words[:, cols].bitcast(FP8X4),
-                scales=q_scales[:, cols],
-                in_=q_grouped[:, cols, :].rearrange("p q j -> p (q j)"),
-            )
+        interleave_on_vector(nc, q_grouped[:, q_halves[0], :], q_raw[:, :, q_halves[0]])
+        interleave_on_scalar(nc, q_grouped[:, q_halves[1], :], q_raw[:, :, q_halves[1]])
+        nc.vector.quantize_mx(
+            out=q_words[:].bitcast(FP8X4), scales=q_scales[:], in_=q_grouped[:].rearrange("p q j -> p (q j)")
+        )
         scores = tile("scores", [P, T], F32)
         for n, cols in enumerate(SCORE_COLS):
             score_sums = bank("score_sums%d" % n, [P, cols.stop - cols.start], n)
@@ -125,30 +139,28 @@ def tile_attend_gatedvalues_heads_kernel(tc, query, keys_words, keys_scales, fac
                 start=True,
                 stop=True,
             )
-            if n == 0:
+            if n < 2:
                 nc.scalar.activation(out=scores[:, cols], in_=score_sums[:], func=ACT.Copy)
             else:
                 nc.vector.tensor_copy(out=scores[:, cols], in_=score_sums[:])
 
+        g0_grouped = tile("g0_grouped", [P, E, PACK], BF16)
+        for u in range(2):
+            pair = slice(2 * u, 2 * u + 2)
+            interleave_on_gpsimd(nc, g0_grouped[:, 0:320, pair], g0_raw[u][:, :, 0:320])
+            interleave_on_scalar(nc, g0_grouped[:, 320:E, pair], g0_raw[u][:, :, 320:E])
+
         listed = tile("listed", [P, SLOTS], F32)
         nc.vector.tensor_copy(out=listed[:], in_=scores[:].indirect(offsets[:]))
-        neg_max = tile("neg_max", [P, 1], F32)
+        neg_max = tile("neg_max", [P, 1], F32, tag="g0_raw1")
         nc.vector.tensor_reduce(out=neg_max[:], in_=listed[:], axis=AXIS.X, op=ALU.max, negate=True)
 
-        g0_grouped = tile("g0_grouped", [P, E, PACK], BF16, tag="k_words")
-        for h, cols in enumerate(GATE_COLS):
-            interleave_on_scalar(nc, g0_grouped[:, cols, :], g0_raw[h][:])
-
-        p_first = tile("p_first", [P, FIRST], F32, tag="g0_raw1")
         p_all = tile("p_all", [P, SLOTS], F32)
         row_sum = tile("row_sum", [P, 1], F32)
         inv_sum = tile("inv_sum", [P, 1], F32)
-        cut = FIRST // PER_COLUMN
-        nc.scalar.activation(out=p_first[:], in_=listed[:, 0:FIRST], func=ACT.Exp, bias=neg_max[:])
         nc.scalar.activation(out=p_all[:], in_=listed[:], func=ACT.Exp, bias=neg_max[:], accum_out=row_sum[:])
-        nc.vector.tensor_copy(out=placed[:].indirect(offsets[:, 0:cut]), in_=p_first[:])
         nc.vector.reciprocal(out=inv_sum[:], in_=row_sum[:])
-        nc.vector.tensor_copy(out=placed[:].indirect(offsets[:, cut : SLOTS // PER_COLUMN]), in_=p_all[:, FIRST:SLOTS])
+        nc.vector.tensor_copy(out=placed[:].indirect(offsets[:]), in_=p_all[:])
 
         fac_half = tile("fac_half", [P, PASSES, PACK], F32)
         nc.gpsimd.tensor_scalar(
@@ -161,31 +173,30 @@ def tile_attend_gatedvalues_heads_kernel(tc, query, keys_words, keys_scales, fac
                 nc.tensor.transpose(rows[:, j, :], fac_half[:, g, j : j + 1].to_broadcast([P, P]), ident[:])
             fac_rows.append(rows)
 
-        v0_grouped = tile("v0_grouped", [P, E, PACK], BF16, tag="listed")
+        g0 = quantise("g0", g0_grouped[:])
+        v0_grouped = tile("v0_grouped", [P, E, PACK], BF16, tag="g0_grouped")
         g1_grouped = tile("g1_grouped", [P, E, PACK], BF16)
         for grouped, raw in ((v0_grouped, v0_raw), (g1_grouped, g1_raw)):
-            for cols in GATE_COLS:
-                interleave_on_scalar(nc, grouped[:, cols, :], raw[:, :, cols])
-        g0 = quantise("g0", g0_grouped[:])
-        v0 = quantise("v0", v0_grouped[:])
-        g1 = quantise("g1", g1_grouped[:])
+            interleave_on_scalar(nc, grouped[:, GATE_COLS[0], :], raw[:, :, GATE_COLS[0]])
+            interleave_on_gpsimd(nc, grouped[:, GATE_COLS[1], :], raw[:, :, GATE_COLS[1]])
 
-        w_pairs = tile("w_pairs", [P, PASSES, 2, 2 * P], BF16, tag="v0_raw")
         w_turned = []
-        for g, reused in enumerate(("g1_raw", "g1_grouped")):
+        w_pairs = tile("w_pairs", [P, PASSES * K_PASS], BF16, offset=0)
+        for g in range(PASSES):
             turned_words = bank("turned_words%d" % g, [P, 2, Q], 6 + g)
             for u in range(2):
                 pair = slice(2 * u, 2 * u + 2)
+                run = w_pairs[:, K_PASS * g + 2 * P * u : K_PASS * g + 2 * P * (u + 1)]
                 nc.vector.scalar_tensor_tensor(
-                    out=w_pairs[:, g, u, :].rearrange("q (p j) -> q p j", j=2),
+                    out=run.rearrange("q (p j) -> q p j", j=2),
                     in0=placed[:, K_PASS * g : K_PASS * (g + 1)].rearrange("q (p j) -> q p j", j=PACK)[:, :, pair],
                     scalar=inv_sum[:],
                     in1=fac_rows[g][:, pair, :].rearrange("q j p -> q p j"),
                     op0=ALU.mult,
                     op1=ALU.mult,
                 )
-                nc.tensor.transpose(turned_words[:, u, :], w_pairs[:, g, u, :].bitcast(F32), ident[:])
-            turned = tile("w_turned%d" % g, [P, Q * PACK], BF16, tag=reused)
+                nc.tensor.transpose(turned_words[:, u, :], run.bitcast(F32), ident[:])
+            turned = tile("w_turned%d" % g, [P, Q * PACK], BF16)
             nc.scalar.copy(
                 out=turned[:].bitcast(F32).rearrange("p (q u) -> p q u", u=2),
                 in_=turned_words[:].rearrange("p u q -> p q u"),
@@ -194,11 +205,13 @@ def tile_attend_gatedvalues_heads_kernel(tc, query, keys_words, keys_scales, fac
         weights = [
             quantise("w%d" % g, w_turned[g][:].rearrange("p (q j) -> p q j", j=PACK)) for g in range(PASSES)
         ]
+        g1 = quantise("g1", g1_grouped[:], offset=2 * T)
+        v0 = quantise("v0", v0_grouped[:], offset=0)
 
-        v1_grouped = tile("v1_grouped", [P, E, PACK], BF16, tag="g1_raw")
-        for cols in OUT_COLS[:2]:
-            interleave_on_vector(nc, v1_grouped[:, cols, :], v1_raw[:, :, cols])
-        interleave_on_scalar(nc, v1_grouped[:, OUT_COLS[2], :], v1_raw[:, :, OUT_COLS[2]])
+        v1_grouped = tile("v1_grouped", [P, E, PACK], BF16)
+        interleave_on_gpsimd(nc, v1_grouped[:, GATE_COLS[0], :], v1_raw[:, :, GATE_COLS[0]])
+        for cols in OUT_COLS[1:]:
+            interleave_on_scalar(nc, v1_grouped[:, cols, :], v1_raw[:, :, cols])
         v1_halves = [quantise("v1_%d" % h, v1_grouped[:, cols, :]) for h, cols in enumerate(GATE_COLS)]
 
         def gate_operand(g, cols):
@@ -218,30 +231,18 @@ def tile_attend_gatedvalues_heads_kernel(tc, query, keys_words, keys_scales, fac
         ]
         products = [(gate_sums[n], gate_operand, cols) for n, cols in enumerate(GATE_COLS)]
         products.extend((value_sums[n], value_operand, cols) for n, cols in enumerate(OUT_COLS))
-        unused_sums = bank("unused_sums", [P, E], 4 + PASSES - 1)
-        for width in (E, QUARTER):
-            nc.tensor.matmul_mx(
-                out=unused_sums[:, 0:width],
-                lhsT=q_words[:].bitcast(FP8X4),
-                lhsT_scale=q_scales[:],
-                rhs=v0[0][:, 0:width].bitcast(FP8X4),
-                rhs_scale=v0[1][:, 0:width],
-                start=True,
-                stop=True,
-            )
-        for run in (products[:3], products[3:]):
-            for g in range(PASSES):
-                for sums, operand, cols in run:
-                    words, scale_bytes = operand(g, cols)
-                    nc.tensor.matmul_mx(
-                        out=sums[:],
-                        lhsT=weights[g][0][:].bitcast(FP8X4),
-                        lhsT_scale=weights[g][1][:],
-                        rhs=words.bitcast(FP8X4),
-                        rhs_scale=scale_bytes,
-                        start=(g == 0),
-                        stop=(g == PASSES - 1),
-                    )
+        for run, g in itertools.product((products[:2], products[2:]), range(PASSES)):
+            for sums, operand, cols in run:
+                words, scale_bytes = operand(g, cols)
+                nc.tensor.matmul_mx(
+                    out=sums[:],
+                    lhsT=weights[g][0][:].bitcast(FP8X4),
+                    lhsT_scale=weights[g][1][:],
+                    rhs=words.bitcast(FP8X4),
+                    rhs_scale=scale_bytes,
+                    start=(g == 0),
+                    stop=(g == PASSES - 1),
+                )
 
         gate = tile("gate", [P, E], F32)
         for n, cols in enumerate(GATE_COLS):

@@ -155,12 +155,16 @@ def tile_attend_gatedvalues_heads_kernel(tc, query, keys_words, keys_scales, fac
         neg_max = tile("neg_max", [P, 1], F32, tag="g0_raw1")
         nc.vector.tensor_reduce(out=neg_max[:], in_=listed[:], axis=AXIS.X, op=ALU.max, negate=True)
 
+        p_first = tile("p_first", [P, FIRST], F32)
         p_all = tile("p_all", [P, SLOTS], F32)
         row_sum = tile("row_sum", [P, 1], F32)
         inv_sum = tile("inv_sum", [P, 1], F32)
+        cut = FIRST // PER_COLUMN
+        nc.scalar.activation(out=p_first[:], in_=listed[:, 0:FIRST], func=ACT.Exp, bias=neg_max[:])
         nc.scalar.activation(out=p_all[:], in_=listed[:], func=ACT.Exp, bias=neg_max[:], accum_out=row_sum[:])
+        nc.vector.tensor_copy(out=placed[:].indirect(offsets[:, 0:cut]), in_=p_first[:])
         nc.vector.reciprocal(out=inv_sum[:], in_=row_sum[:])
-        nc.vector.tensor_copy(out=placed[:].indirect(offsets[:]), in_=p_all[:])
+        nc.vector.tensor_copy(out=placed[:].indirect(offsets[:, cut : SLOTS // PER_COLUMN]), in_=p_all[:, FIRST:SLOTS])
 
         fac_half = tile("fac_half", [P, PASSES, PACK], F32)
         nc.gpsimd.tensor_scalar(
@@ -168,9 +172,9 @@ def tile_attend_gatedvalues_heads_kernel(tc, query, keys_words, keys_scales, fac
         )
         fac_rows = []
         for g in range(PASSES):
-            rows = bank("fac_rows%d" % g, [P, PACK, P], 4 + g)
+            rows = bank("fac_rows%d" % g, [P, 2, P, 2], 4 + g)
             for j in range(PACK):
-                nc.tensor.transpose(rows[:, j, :], fac_half[:, g, j : j + 1].to_broadcast([P, P]), ident[:])
+                nc.tensor.transpose(rows[:, j // 2, :, j % 2], fac_half[:, g, j : j + 1].to_broadcast([P, P]), ident[:])
             fac_rows.append(rows)
 
         g0 = quantise("g0", g0_grouped[:])
@@ -191,7 +195,7 @@ def tile_attend_gatedvalues_heads_kernel(tc, query, keys_words, keys_scales, fac
                     out=run.rearrange("q (p j) -> q p j", j=2),
                     in0=placed[:, K_PASS * g : K_PASS * (g + 1)].rearrange("q (p j) -> q p j", j=PACK)[:, :, pair],
                     scalar=inv_sum[:],
-                    in1=fac_rows[g][:, pair, :].rearrange("q j p -> q p j"),
+                    in1=fac_rows[g][:, u, :, :],
                     op0=ALU.mult,
                     op1=ALU.mult,
                 )

@@ -27,8 +27,16 @@ PER_COLUMN = 16
 LINE = 4
 HALF = E // 2
 QUARTER = E // 4
+UNLISTED = -(2.0**127)
+KIB = 1024
+V0_CUT = 288
+AT_G1B = 0
+AT_G1A = 4 * KIB
+AT_V0 = 8 * KIB
+AT_PAIRS = (16 * KIB, 19 * KIB)
+AT_TURNED = 21 * KIB
 FIRST = 128
-SCORE_COLS = (slice(0, 256), slice(256, 512), slice(512, 768), slice(768, 1024))
+SCORE_COLS = (slice(0, 256), slice(256, 512), slice(512, 768), slice(768, 896), slice(896, 1024))
 GATE_COLS = (slice(0, HALF), slice(HALF, E))
 OUT_COLS = (slice(0, HALF), slice(HALF, HALF + QUARTER), slice(HALF + QUARTER, E))
 
@@ -75,18 +83,9 @@ def tile_attend_gatedvalues_heads_kernel(tc, query, keys_words, keys_scales, fac
             nc.sync.dma_start(out=raw[:], in_=rows[:, :, cols])
             return raw
 
-        def load_pairs(name, source, g):
-            rows = source[K_PASS * g : K_PASS * (g + 1), :].rearrange("(p u j) e -> p u j e", u=2, j=2)
-            pairs = []
-            for u in range(2):
-                raw = tile("%s%d" % (name, u), [P, 2, E], F32)
-                nc.sync.dma_start(out=raw[:], in_=rows[:, u, :, :])
-                pairs.append(raw)
-            return pairs
-
-        def quantise(name, grouped, tag=None, offset=None):
-            words = tile(name + "_words", [P, grouped.shape[1]], U32, tag=tag, offset=offset)
-            scale_bytes = tile(name + "_scales", [P, grouped.shape[1]], U8)
+        def quantise(name, grouped, offset=None, scales_offset=None):
+            words = tile(name + "_words", [P, grouped.shape[1]], U32, offset=offset)
+            scale_bytes = tile(name + "_scales", [P, grouped.shape[1]], U8, offset=scales_offset)
             nc.vector.quantize_mx(
                 out=words[:].bitcast(FP8X4), scales=scale_bytes[:], in_=grouped.rearrange("p x j -> p (x j)")
             )
@@ -106,17 +105,19 @@ def tile_attend_gatedvalues_heads_kernel(tc, query, keys_words, keys_scales, fac
                 in_=keys_scales[0, 4 * quad : 4 * quad + 4, :].bitcast(I32),
             )
         nc.sync.dma_start(offsets[:], offs)
-        g0_raw = load_pairs("g0_raw", gval, 0)
+        g0_raw = load_pass("g0_raw", gval, 0, slice(0, E))
         nc.sync.dma_start(out=fac_raw[:, :, 0:PACK], in_=fac.rearrange("o (g p j) -> p (o g) j", g=PASSES, j=PACK))
-        v0_raw = load_pass("v0_raw", vals, 0, slice(0, E))
-        g1_raw = load_pass("g1_raw", gval, 1, slice(0, E), offset=0)
-        v1_raw = load_pass("v1_raw", vals, 1, slice(0, E))
+        v0_raw = load_pass("v0_raw", vals, 0, slice(0, E), offset=AT_V0)
+        g1_raw = [
+            load_pass("g1_raw%d" % h, gval, 1, GATE_COLS[h], offset=(AT_G1A, AT_G1B)[h]) for h in range(2)
+        ]
+        v1_raw = [load_pass("v1_raw%d" % h, vals, 1, GATE_COLS[h]) for h in range(2)]
 
         ident = tile("ident", [P, P], F32)
         nc.vector.memset(ident[:], 0.0)
         make_identity(nc, ident[:], nomemset=True)
         placed = tile("placed", [P, T], F32)
-        nc.vector.memset(placed[:], 0.0)
+        nc.vector.memset(placed[:], UNLISTED)
 
         q_grouped = tile("q_grouped", [P, Q, PACK], BF16)
         q_words = tile("q_words", [P, Q], U32)
@@ -129,7 +130,7 @@ def tile_attend_gatedvalues_heads_kernel(tc, query, keys_words, keys_scales, fac
         )
         scores = tile("scores", [P, T], F32)
         for n, cols in enumerate(SCORE_COLS):
-            score_sums = bank("score_sums%d" % n, [P, cols.stop - cols.start], n)
+            score_sums = bank("score_sums%d" % n, [P, cols.stop - cols.start], (n + 6) % 8)
             nc.tensor.matmul_mx(
                 out=score_sums[:],
                 lhsT=q_words[:].bitcast(FP8X4),
@@ -139,32 +140,26 @@ def tile_attend_gatedvalues_heads_kernel(tc, query, keys_words, keys_scales, fac
                 start=True,
                 stop=True,
             )
-            if n < 2:
+            if n % 2 == 0:
                 nc.scalar.activation(out=scores[:, cols], in_=score_sums[:], func=ACT.Copy)
             else:
                 nc.vector.tensor_copy(out=scores[:, cols], in_=score_sums[:])
 
         g0_grouped = tile("g0_grouped", [P, E, PACK], BF16)
-        for u in range(2):
-            pair = slice(2 * u, 2 * u + 2)
-            interleave_on_gpsimd(nc, g0_grouped[:, 0:320, pair], g0_raw[u][:, :, 0:320])
-            interleave_on_scalar(nc, g0_grouped[:, 320:E, pair], g0_raw[u][:, :, 320:E])
+        interleave_on_scalar(nc, g0_grouped[:, GATE_COLS[0], :], g0_raw[:, :, GATE_COLS[0]])
+        interleave_on_gpsimd(nc, g0_grouped[:, GATE_COLS[1], :], g0_raw[:, :, GATE_COLS[1]])
 
+        columns = SLOTS // PER_COLUMN
         listed = tile("listed", [P, SLOTS], F32)
-        nc.vector.tensor_copy(out=listed[:], in_=scores[:].indirect(offsets[:]))
-        neg_max = tile("neg_max", [P, 1], F32, tag="g0_raw1")
-        nc.vector.tensor_reduce(out=neg_max[:], in_=listed[:], axis=AXIS.X, op=ALU.max, negate=True)
-
-        p_first = tile("p_first", [P, FIRST], F32)
-        p_all = tile("p_all", [P, SLOTS], F32)
-        row_sum = tile("row_sum", [P, 1], F32)
-        inv_sum = tile("inv_sum", [P, 1], F32)
+        for part in (slice(0, columns // 2), slice(columns // 2, columns)):
+            nc.vector.tensor_copy(
+                out=listed[:, PER_COLUMN * part.start : PER_COLUMN * part.stop], in_=scores[:].indirect(offsets[:, part])
+            )
         cut = FIRST // PER_COLUMN
-        nc.scalar.activation(out=p_first[:], in_=listed[:, 0:FIRST], func=ACT.Exp, bias=neg_max[:])
-        nc.scalar.activation(out=p_all[:], in_=listed[:], func=ACT.Exp, bias=neg_max[:], accum_out=row_sum[:])
-        nc.vector.tensor_copy(out=placed[:].indirect(offsets[:, 0:cut]), in_=p_first[:])
-        nc.vector.reciprocal(out=inv_sum[:], in_=row_sum[:])
-        nc.vector.tensor_copy(out=placed[:].indirect(offsets[:, cut : SLOTS // PER_COLUMN]), in_=p_all[:, FIRST:SLOTS])
+        neg_max = tile("neg_max", [P, 1], F32)
+        nc.vector.tensor_copy(out=placed[:].indirect(offsets[:, 0:cut]), in_=listed[:, 0:FIRST])
+        nc.vector.tensor_reduce(out=neg_max[:], in_=listed[:], axis=AXIS.X, op=ALU.max, negate=True)
+        nc.vector.tensor_copy(out=placed[:].indirect(offsets[:, cut:columns]), in_=listed[:, FIRST:SLOTS])
 
         fac_half = tile("fac_half", [P, PASSES, PACK], F32)
         nc.gpsimd.tensor_scalar(
@@ -177,55 +172,82 @@ def tile_attend_gatedvalues_heads_kernel(tc, query, keys_words, keys_scales, fac
                 nc.tensor.transpose(rows[:, j // 2, :, j % 2], fac_half[:, g, j : j + 1].to_broadcast([P, P]), ident[:])
             fac_rows.append(rows)
 
-        g0 = quantise("g0", g0_grouped[:])
-        v0_grouped = tile("v0_grouped", [P, E, PACK], BF16, tag="g0_grouped")
-        g1_grouped = tile("g1_grouped", [P, E, PACK], BF16)
-        for grouped, raw in ((v0_grouped, v0_raw), (g1_grouped, g1_raw)):
-            interleave_on_scalar(nc, grouped[:, GATE_COLS[0], :], raw[:, :, GATE_COLS[0]])
-            interleave_on_gpsimd(nc, grouped[:, GATE_COLS[1], :], raw[:, :, GATE_COLS[1]])
+        v0_grouped = tile("v0_grouped", [P, E, PACK], BF16)
+        interleave_on_scalar(nc, v0_grouped[:, 0:V0_CUT, :], v0_raw[:, :, 0:V0_CUT])
+        interleave_on_gpsimd(nc, v0_grouped[:, V0_CUT:E, :], v0_raw[:, :, V0_CUT:E])
+
+        p_listed = tile("p_listed", [P, SLOTS], F32, offset=AT_V0)
+        row_sum = tile("row_sum", [P, 1], F32)
+        inv_sum = tile("inv_sum", [P, 1], F32)
+        nc.scalar.activation(out=p_listed[:], in_=listed[:], func=ACT.Exp, bias=neg_max[:], accum_out=row_sum[:])
+        nc.vector.reciprocal(out=inv_sum[:], in_=row_sum[:])
+
+        g1_grouped = tile("g1_grouped", [P, HALF + QUARTER, PACK], BF16)
+        interleave_on_gpsimd(nc, g1_grouped[:, GATE_COLS[0], :], g1_raw[0][:])
+        interleave_on_scalar(nc, g1_grouped[:, OUT_COLS[1], :], g1_raw[1][:, :, 0:QUARTER])
+        g0 = quantise("g0", g0_grouped[:], offset=AT_G1A)
+        g1_last = tile("g1_last", [P, QUARTER, PACK], BF16, tag="g0_grouped")
+        interleave_on_gpsimd(nc, g1_last[:], g1_raw[1][:, :, QUARTER:HALF])
+        v1_grouped = [tile("v1_grouped0", [P, HALF, PACK], BF16)]
+        interleave_on_gpsimd(nc, v1_grouped[0][:, 0:QUARTER, :], v1_raw[0][:, :, 0:QUARTER])
+
+        p_placed = tile("p_placed", [P, PASSES, 2, P, 2], F32, offset=AT_V0 + 2 * KIB)
+        for g, u in itertools.product(range(PASSES), range(2)):
+            tokens = placed[:, K_PASS * g : K_PASS * (g + 1)].rearrange("q (p j) -> q p j", j=PACK)
+            nc.scalar.activation(
+                out=p_placed[:, g, u, :, :], in_=tokens[:, :, 2 * u : 2 * u + 2], func=ACT.Exp, bias=neg_max[:]
+            )
+        interleave_on_scalar(nc, v1_grouped[0][:, QUARTER:HALF, :], v1_raw[0][:, :, QUARTER:HALF])
 
         w_turned = []
-        w_pairs = tile("w_pairs", [P, PASSES * K_PASS], BF16, offset=0)
         for g in range(PASSES):
+            w_pairs = tile("w_pairs%d" % g, [P, K_PASS], BF16, offset=AT_PAIRS[g])
             turned_words = bank("turned_words%d" % g, [P, 2, Q], 6 + g)
             for u in range(2):
-                pair = slice(2 * u, 2 * u + 2)
-                run = w_pairs[:, K_PASS * g + 2 * P * u : K_PASS * g + 2 * P * (u + 1)]
+                run = w_pairs[:, 2 * P * u : 2 * P * (u + 1)]
                 nc.vector.scalar_tensor_tensor(
                     out=run.rearrange("q (p j) -> q p j", j=2),
-                    in0=placed[:, K_PASS * g : K_PASS * (g + 1)].rearrange("q (p j) -> q p j", j=PACK)[:, :, pair],
+                    in0=p_placed[:, g, u, :, :],
                     scalar=inv_sum[:],
                     in1=fac_rows[g][:, u, :, :],
                     op0=ALU.mult,
                     op1=ALU.mult,
                 )
                 nc.tensor.transpose(turned_words[:, u, :], run.bitcast(F32), ident[:])
-            turned = tile("w_turned%d" % g, [P, Q * PACK], BF16)
+            turned = tile("w_turned%d" % g, [P, Q * PACK], BF16, offset=AT_TURNED + KIB * g)
             nc.scalar.copy(
                 out=turned[:].bitcast(F32).rearrange("p (q u) -> p q u", u=2),
                 in_=turned_words[:].rearrange("p u q -> p q u"),
             )
             w_turned.append(turned)
+        g1 = (tile("g1_words", [P, E], U32, offset=AT_PAIRS[0]), tile("g1_scales", [P, E], U8))
+        for cols, grouped in zip(OUT_COLS, (g1_grouped[:, OUT_COLS[0], :], g1_grouped[:, OUT_COLS[1], :], g1_last[:])):
+            nc.vector.quantize_mx(
+                out=g1[0][:, cols].bitcast(FP8X4), scales=g1[1][:, cols], in_=grouped.rearrange("p x j -> p (x j)")
+            )
+        for n in (1, 2):
+            at = AT_PAIRS[1] + KIB * (n - 1) - KIB // 2
+            v1_grouped.append(tile("v1_grouped%d" % n, [P, QUARTER, PACK], BF16, offset=at))
+            interleave_on_scalar(nc, v1_grouped[n][:], v1_raw[1][:, :, QUARTER * (n - 1) : QUARTER * n])
         weights = [
             quantise("w%d" % g, w_turned[g][:].rearrange("p (q j) -> p q j", j=PACK)) for g in range(PASSES)
         ]
-        g1 = quantise("g1", g1_grouped[:], offset=2 * T)
-        v0 = quantise("v0", v0_grouped[:], offset=0)
-
-        v1_grouped = tile("v1_grouped", [P, E, PACK], BF16)
-        interleave_on_gpsimd(nc, v1_grouped[:, GATE_COLS[0], :], v1_raw[:, :, GATE_COLS[0]])
-        for cols in OUT_COLS[1:]:
-            interleave_on_scalar(nc, v1_grouped[:, cols, :], v1_raw[:, :, cols])
-        v1_halves = [quantise("v1_%d" % h, v1_grouped[:, cols, :]) for h, cols in enumerate(GATE_COLS)]
+        v0_first = quantise("v0_0", v0_grouped[:, GATE_COLS[0], :], scales_offset=AT_TURNED)
+        v1_pieces = [quantise("v1_0", v1_grouped[0][:], scales_offset=AT_TURNED + HALF)]
+        v0_halves = [v0_first, quantise("v0_1", v0_grouped[:, GATE_COLS[1], :], scales_offset=AT_TURNED + 2 * HALF)]
+        for n in (1, 2):
+            at = AT_TURNED + 3 * HALF + QUARTER * (n - 1)
+            v1_pieces.append(quantise("v1_%d" % n, v1_grouped[n][:], scales_offset=at))
 
         def gate_operand(g, cols):
             words, scale_bytes = (g0, g1)[g]
             return words[:, cols], scale_bytes[:, cols]
 
         def value_operand(g, cols):
-            if g == 0:
-                return v0[0][:, cols], v0[1][:, cols]
-            words, scale_bytes = v1_halves[cols.start // HALF]
+            if g == 1:
+                words, scale_bytes = v1_pieces[OUT_COLS.index(cols)]
+                return words[:], scale_bytes[:]
+            words, scale_bytes = v0_halves[cols.start // HALF]
             inside = slice(cols.start % HALF, cols.start % HALF + cols.stop - cols.start)
             return words[:, inside], scale_bytes[:, inside]
 
@@ -235,7 +257,8 @@ def tile_attend_gatedvalues_heads_kernel(tc, query, keys_words, keys_scales, fac
         ]
         products = [(gate_sums[n], gate_operand, cols) for n, cols in enumerate(GATE_COLS)]
         products.extend((value_sums[n], value_operand, cols) for n, cols in enumerate(OUT_COLS))
-        for run, g in itertools.product((products[:2], products[2:]), range(PASSES)):
+        runs = (products[:2], products[2:3], products[3:4], products[4:])
+        for run, g in itertools.product(runs, range(PASSES)):
             for sums, operand, cols in run:
                 words, scale_bytes = operand(g, cols)
                 nc.tensor.matmul_mx(

@@ -29,12 +29,12 @@ HALF = E // 2
 QUARTER = E // 4
 UNLISTED = -(2.0**127)
 KIB = 1024
+ALIGN = 64
 V0_CUT = 288
-AT_G1B = 0
-AT_G1A = 4 * KIB
-AT_V0 = 8 * KIB
-AT_PAIRS = (16 * KIB, 19 * KIB)
-AT_TURNED = 21 * KIB
+G1_CUT = 96
+AT_V0 = 0
+AT_G1 = 8 * KIB
+AT_TURNED = 24 * KIB
 FIRST = 128
 SCORE_COLS = (slice(0, 256), slice(256, 512), slice(512, 768), slice(768, 896), slice(896, 1024))
 GATE_COLS = (slice(0, HALF), slice(HALF, E))
@@ -108,10 +108,8 @@ def tile_attend_gatedvalues_heads_kernel(tc, query, keys_words, keys_scales, fac
         g0_raw = load_pass("g0_raw", gval, 0, slice(0, E))
         nc.sync.dma_start(out=fac_raw[:, :, 0:PACK], in_=fac.rearrange("o (g p j) -> p (o g) j", g=PASSES, j=PACK))
         v0_raw = load_pass("v0_raw", vals, 0, slice(0, E), offset=AT_V0)
-        g1_raw = [
-            load_pass("g1_raw%d" % h, gval, 1, GATE_COLS[h], offset=(AT_G1A, AT_G1B)[h]) for h in range(2)
-        ]
-        v1_raw = [load_pass("v1_raw%d" % h, vals, 1, GATE_COLS[h]) for h in range(2)]
+        g1_raw = load_pass("g1_raw", gval, 1, slice(0, E), offset=AT_G1)
+        v1_raw = load_pass("v1_raw", vals, 1, slice(0, E))
 
         ident = tile("ident", [P, P], F32)
         nc.vector.memset(ident[:], 0.0)
@@ -176,78 +174,89 @@ def tile_attend_gatedvalues_heads_kernel(tc, query, keys_words, keys_scales, fac
         interleave_on_scalar(nc, v0_grouped[:, 0:V0_CUT, :], v0_raw[:, :, 0:V0_CUT])
         interleave_on_gpsimd(nc, v0_grouped[:, V0_CUT:E, :], v0_raw[:, :, V0_CUT:E])
 
-        p_listed = tile("p_listed", [P, SLOTS], F32, offset=AT_V0)
-        row_sum = tile("row_sum", [P, 1], F32)
+        p_listed = tile("p_listed", [P, SLOTS], F32, offset=AT_V0 + KIB)
+        row_sum = tile("row_sum", [P, 1], F32)[:]
         inv_sum = tile("inv_sum", [P, 1], F32)
-        nc.scalar.activation(out=p_listed[:], in_=listed[:], func=ACT.Exp, bias=neg_max[:], accum_out=row_sum[:])
-        nc.vector.reciprocal(out=inv_sum[:], in_=row_sum[:])
+        nc.scalar.activation(out=p_listed[:], in_=listed[:], func=ACT.Exp, bias=neg_max[:], accum_out=row_sum)
+        nc.vector.reciprocal(out=inv_sum[:], in_=row_sum)
 
-        g1_grouped = tile("g1_grouped", [P, HALF + QUARTER, PACK], BF16)
-        interleave_on_gpsimd(nc, g1_grouped[:, GATE_COLS[0], :], g1_raw[0][:])
-        interleave_on_scalar(nc, g1_grouped[:, OUT_COLS[1], :], g1_raw[1][:, :, 0:QUARTER])
-        g0 = quantise("g0", g0_grouped[:], offset=AT_G1A)
-        g1_last = tile("g1_last", [P, QUARTER, PACK], BF16, tag="g0_grouped")
-        interleave_on_gpsimd(nc, g1_last[:], g1_raw[1][:, :, QUARTER:HALF])
-        v1_grouped = [tile("v1_grouped0", [P, HALF, PACK], BF16)]
-        interleave_on_gpsimd(nc, v1_grouped[0][:, 0:QUARTER, :], v1_raw[0][:, :, 0:QUARTER])
+        g1_grouped = [None, tile("g1_grouped1", [P, HALF, PACK], BF16)]
+        interleave_on_gpsimd(nc, g1_grouped[1][:, 0:G1_CUT, :], g1_raw[:, :, HALF : HALF + G1_CUT])
+        g0 = quantise("g0", g0_grouped[:], offset=AT_V0)
+        g1_grouped[0] = tile("g1_grouped0", [P, HALF, PACK], BF16, tag="g0_grouped")
+        interleave_on_gpsimd(nc, g1_grouped[0][:], g1_raw[:, :, GATE_COLS[0]])
 
-        p_placed = tile("p_placed", [P, PASSES, 2, P, 2], F32, offset=AT_V0 + 2 * KIB)
+        p_placed = {}
         for g, u in itertools.product(range(PASSES), range(2)):
+            p_placed[g, u] = tile("p_placed%d%d" % (g, u), [P, 2 * P], F32, offset=AT_V0 + (3 + 2 * g + u) * KIB)
             tokens = placed[:, K_PASS * g : K_PASS * (g + 1)].rearrange("q (p j) -> q p j", j=PACK)
             nc.scalar.activation(
-                out=p_placed[:, g, u, :, :], in_=tokens[:, :, 2 * u : 2 * u + 2], func=ACT.Exp, bias=neg_max[:]
+                out=p_placed[g, u][:].rearrange("q (p j) -> q p j", j=2),
+                in_=tokens[:, :, 2 * u : 2 * u + 2],
+                func=ACT.Exp,
+                bias=neg_max[:],
             )
-        interleave_on_scalar(nc, v1_grouped[0][:, QUARTER:HALF, :], v1_raw[0][:, :, QUARTER:HALF])
+        interleave_on_scalar(nc, g1_grouped[1][:, G1_CUT:HALF, :], g1_raw[:, :, HALF + G1_CUT : E])
 
         w_turned = []
+        v1_grouped = [tile("v1_grouped0", [P, QUARTER, PACK], BF16)]
         for g in range(PASSES):
-            w_pairs = tile("w_pairs%d" % g, [P, K_PASS], BF16, offset=AT_PAIRS[g])
+            w_pairs = tile("w_pairs%d" % g, [P, K_PASS], BF16)
             turned_words = bank("turned_words%d" % g, [P, 2, Q], 6 + g)
             for u in range(2):
                 run = w_pairs[:, 2 * P * u : 2 * P * (u + 1)]
                 nc.vector.scalar_tensor_tensor(
-                    out=run.rearrange("q (p j) -> q p j", j=2),
-                    in0=p_placed[:, g, u, :, :],
+                    out=run,
+                    in0=p_placed[g, u][:],
                     scalar=inv_sum[:],
-                    in1=fac_rows[g][:, u, :, :],
+                    in1=fac_rows[g][:, u, :, :].rearrange("q p j -> q (p j)"),
                     op0=ALU.mult,
                     op1=ALU.mult,
                 )
                 nc.tensor.transpose(turned_words[:, u, :], run.bitcast(F32), ident[:])
-            turned = tile("w_turned%d" % g, [P, Q * PACK], BF16, offset=AT_TURNED + KIB * g)
+            turned = tile("w_turned%d" % g, [P, Q * PACK], BF16, offset=AT_TURNED + 2 * KIB * g)
             nc.scalar.copy(
                 out=turned[:].bitcast(F32).rearrange("p (q u) -> p q u", u=2),
                 in_=turned_words[:].rearrange("p u q -> p q u"),
             )
-            w_turned.append(turned)
-        g1 = (tile("g1_words", [P, E], U32, offset=AT_PAIRS[0]), tile("g1_scales", [P, E], U8))
-        for cols, grouped in zip(OUT_COLS, (g1_grouped[:, OUT_COLS[0], :], g1_grouped[:, OUT_COLS[1], :], g1_last[:])):
-            nc.vector.quantize_mx(
-                out=g1[0][:, cols].bitcast(FP8X4), scales=g1[1][:, cols], in_=grouped.rearrange("p x j -> p (x j)")
-            )
-        for n in (1, 2):
-            at = AT_PAIRS[1] + KIB * (n - 1) - KIB // 2
-            v1_grouped.append(tile("v1_grouped%d" % n, [P, QUARTER, PACK], BF16, offset=at))
-            interleave_on_scalar(nc, v1_grouped[n][:], v1_raw[1][:, :, QUARTER * (n - 1) : QUARTER * n])
-        weights = [
-            quantise("w%d" % g, w_turned[g][:].rearrange("p (q j) -> p q j", j=PACK)) for g in range(PASSES)
+            w_turned.append(turned[:].rearrange("p (q j) -> p q j", j=PACK))
+            if g == 0:
+                interleave_on_scalar(nc, v1_grouped[0][:], v1_raw[:, :, 0:QUARTER])
+        third_run = AT_V0 + 5 * KIB
+        v0 = [quantise("v0_0", v0_grouped[:, GATE_COLS[0], :], scales_offset=third_run)]
+        g1 = [quantise("g1_0", g1_grouped[0][:], scales_offset=third_run + HALF)]
+        weights = [quantise("w0", w_turned[0])]
+        v1_grouped.append(tile("v1_grouped1", [P, QUARTER, PACK], BF16, offset=AT_TURNED + KIB - ALIGN))
+        interleave_on_vector(nc, v1_grouped[1][:], v1_raw[:, :, QUARTER:HALF])
+        for n in (2, 3):
+            v1_grouped.append(tile("v1_grouped%d" % n, [P, QUARTER, PACK], BF16))
+            interleave_on_scalar(nc, v1_grouped[n][:], v1_raw[:, :, OUT_COLS[n - 1]])
+        weights.append(quantise("w1", w_turned[1], scales_offset=AT_TURNED + ALIGN))
+        g1.append(quantise("g1_1", g1_grouped[1][:], scales_offset=AT_TURNED + HALF))
+        v1_pieces = [
+            (tile("v1_0_words", [P, HALF], U32), tile("v1_0_scales", [P, HALF], U8, offset=AT_TURNED - HALF + ALIGN))
         ]
-        v0_first = quantise("v0_0", v0_grouped[:, GATE_COLS[0], :], scales_offset=AT_TURNED)
-        v1_pieces = [quantise("v1_0", v1_grouped[0][:], scales_offset=AT_TURNED + HALF)]
-        v0_halves = [v0_first, quantise("v0_1", v0_grouped[:, GATE_COLS[1], :], scales_offset=AT_TURNED + 2 * HALF)]
-        for n in (1, 2):
-            at = AT_TURNED + 3 * HALF + QUARTER * (n - 1)
-            v1_pieces.append(quantise("v1_%d" % n, v1_grouped[n][:], scales_offset=at))
+        for n in range(2):
+            cols = slice(QUARTER * n, QUARTER * (n + 1))
+            nc.vector.quantize_mx(
+                out=v1_pieces[0][0][:, cols].bitcast(FP8X4),
+                scales=v1_pieces[0][1][:, cols],
+                in_=v1_grouped[n][:].rearrange("p x j -> p (x j)"),
+            )
+        v0.append(quantise("v0_1", v0_grouped[:, GATE_COLS[1], :], scales_offset=AT_TURNED + 2 * HALF))
+        v1_pieces.extend(quantise("v1_%d" % n, v1_grouped[n][:]) for n in (2, 3))
 
         def gate_operand(g, cols):
-            words, scale_bytes = (g0, g1)[g]
-            return words[:, cols], scale_bytes[:, cols]
+            if g == 1:
+                words, scale_bytes = g1[GATE_COLS.index(cols)]
+                return words[:], scale_bytes[:]
+            return g0[0][:, cols], g0[1][:, cols]
 
         def value_operand(g, cols):
             if g == 1:
                 words, scale_bytes = v1_pieces[OUT_COLS.index(cols)]
                 return words[:], scale_bytes[:]
-            words, scale_bytes = v0_halves[cols.start // HALF]
+            words, scale_bytes = v0[cols.start // HALF]
             inside = slice(cols.start % HALF, cols.start % HALF + cols.stop - cols.start)
             return words[:, inside], scale_bytes[:, inside]
 

@@ -31,7 +31,8 @@ UNLISTED = -(2.0**127)
 KIB = 1024
 ALIGN = 64
 V0_CUT = 288
-G1_CUT = 96
+G1_CUTS = (slice(0, 96), slice(96, 160), slice(160, 256))
+LAST_CUT = 96
 AT_V0 = 0
 AT_G1 = 8 * KIB
 AT_TURNED = 24 * KIB
@@ -181,8 +182,12 @@ def tile_attend_gatedvalues_heads_kernel(tc, query, keys_words, keys_scales, fac
         nc.vector.reciprocal(out=inv_sum[:], in_=row_sum)
 
         g1_grouped = [None, tile("g1_grouped1", [P, HALF, PACK], BF16)]
-        interleave_on_gpsimd(nc, g1_grouped[1][:, 0:G1_CUT, :], g1_raw[:, :, HALF : HALF + G1_CUT])
-        g0 = quantise("g0", g0_grouped[:], offset=AT_V0)
+        interleave_on_gpsimd(nc, g1_grouped[1][:, G1_CUTS[0], :], g1_raw[:, :, HALF:E][:, :, G1_CUTS[0]])
+        g0 = [
+            quantise("g0_%d" % h, g0_grouped[:, cols, :], scales_offset=AT_V0 + KIB + HALF * h)
+            for h, cols in enumerate(GATE_COLS)
+        ]
+        v0_third = quantise("v0_1", v0_grouped[:, OUT_COLS[1], :], scales_offset=AT_V0 + 2 * KIB)
         g1_grouped[0] = tile("g1_grouped0", [P, HALF, PACK], BF16, tag="g0_grouped")
         interleave_on_gpsimd(nc, g1_grouped[0][:], g1_raw[:, :, GATE_COLS[0]])
 
@@ -196,10 +201,9 @@ def tile_attend_gatedvalues_heads_kernel(tc, query, keys_words, keys_scales, fac
                 func=ACT.Exp,
                 bias=neg_max[:],
             )
-        interleave_on_scalar(nc, g1_grouped[1][:, G1_CUT:HALF, :], g1_raw[:, :, HALF + G1_CUT : E])
+        interleave_on_scalar(nc, g1_grouped[1][:, G1_CUTS[1], :], g1_raw[:, :, HALF:E][:, :, G1_CUTS[1]])
 
         w_turned = []
-        v1_grouped = [tile("v1_grouped0", [P, QUARTER, PACK], BF16)]
         for g in range(PASSES):
             w_pairs = tile("w_pairs%d" % g, [P, K_PASS], BF16)
             turned_words = bank("turned_words%d" % g, [P, 2, Q], 6 + g)
@@ -221,44 +225,36 @@ def tile_attend_gatedvalues_heads_kernel(tc, query, keys_words, keys_scales, fac
             )
             w_turned.append(turned[:].rearrange("p (q j) -> p q j", j=PACK))
             if g == 0:
-                interleave_on_scalar(nc, v1_grouped[0][:], v1_raw[:, :, 0:QUARTER])
+                interleave_on_scalar(nc, g1_grouped[1][:, G1_CUTS[2], :], g1_raw[:, :, HALF:E][:, :, G1_CUTS[2]])
         third_run = AT_V0 + 5 * KIB
         v0 = [quantise("v0_0", v0_grouped[:, GATE_COLS[0], :], scales_offset=third_run)]
-        g1 = [quantise("g1_0", g1_grouped[0][:], scales_offset=third_run + HALF)]
         weights = [quantise("w0", w_turned[0])]
-        v1_grouped.append(tile("v1_grouped1", [P, QUARTER, PACK], BF16, offset=AT_TURNED + KIB - ALIGN))
-        interleave_on_vector(nc, v1_grouped[1][:], v1_raw[:, :, QUARTER:HALF])
-        for n in (2, 3):
-            v1_grouped.append(tile("v1_grouped%d" % n, [P, QUARTER, PACK], BF16))
-            interleave_on_scalar(nc, v1_grouped[n][:], v1_raw[:, :, OUT_COLS[n - 1]])
-        weights.append(quantise("w1", w_turned[1], scales_offset=AT_TURNED + ALIGN))
-        g1.append(quantise("g1_1", g1_grouped[1][:], scales_offset=AT_TURNED + HALF))
-        v1_pieces = [
-            (tile("v1_0_words", [P, HALF], U32), tile("v1_0_scales", [P, HALF], U8, offset=AT_TURNED - HALF + ALIGN))
+        g1 = [quantise("g1_0", g1_grouped[0][:], scales_offset=AT_TURNED + ALIGN)]
+        v1_grouped = [
+            tile("v1_grouped0", [P, HALF, PACK], BF16, offset=AT_TURNED + ALIGN - 2 * KIB),
+            tile("v1_grouped1", [P, QUARTER, PACK], BF16),
+            tile("v1_grouped2", [P, QUARTER, PACK], BF16, offset=AT_TURNED + KIB - ALIGN),
         ]
-        for n in range(2):
-            cols = slice(QUARTER * n, QUARTER * (n + 1))
-            nc.vector.quantize_mx(
-                out=v1_pieces[0][0][:, cols].bitcast(FP8X4),
-                scales=v1_pieces[0][1][:, cols],
-                in_=v1_grouped[n][:].rearrange("p x j -> p (x j)"),
-            )
-        v0.append(quantise("v0_1", v0_grouped[:, GATE_COLS[1], :], scales_offset=AT_TURNED + 2 * HALF))
-        v1_pieces.extend(quantise("v1_%d" % n, v1_grouped[n][:]) for n in (2, 3))
+        v1_last = v1_raw[:, :, OUT_COLS[2]]
+        interleave_on_scalar(nc, v1_grouped[0][:, 0:QUARTER, :], v1_raw[:, :, 0:QUARTER])
+        interleave_on_scalar(nc, v1_grouped[1][:], v1_raw[:, :, OUT_COLS[1]])
+        interleave_on_scalar(nc, v1_grouped[2][:, 0:LAST_CUT, :], v1_last[:, :, 0:LAST_CUT])
+        interleave_on_vector(nc, v1_grouped[0][:, QUARTER:HALF, :], v1_raw[:, :, QUARTER:HALF])
+        at = AT_TURNED + ALIGN + HALF
+        weights.append(quantise("w1", w_turned[1], scales_offset=at))
+        g1.append(quantise("g1_1", g1_grouped[1][:], scales_offset=at + QUARTER))
+        interleave_on_vector(nc, v1_grouped[2][:, LAST_CUT:QUARTER, :], v1_last[:, :, LAST_CUT:QUARTER])
+        v1_pieces = [quantise("v1_0", v1_grouped[0][:])]
+        v0.extend((v0_third, quantise("v0_2", v0_grouped[:, OUT_COLS[2], :], scales_offset=at + QUARTER + HALF)))
+        v1_pieces.extend(quantise("v1_%d" % n, v1_grouped[n][:]) for n in (1, 2))
 
         def gate_operand(g, cols):
-            if g == 1:
-                words, scale_bytes = g1[GATE_COLS.index(cols)]
-                return words[:], scale_bytes[:]
-            return g0[0][:, cols], g0[1][:, cols]
+            words, scale_bytes = (g0, g1)[g][GATE_COLS.index(cols)]
+            return words[:], scale_bytes[:]
 
         def value_operand(g, cols):
-            if g == 1:
-                words, scale_bytes = v1_pieces[OUT_COLS.index(cols)]
-                return words[:], scale_bytes[:]
-            words, scale_bytes = v0[cols.start // HALF]
-            inside = slice(cols.start % HALF, cols.start % HALF + cols.stop - cols.start)
-            return words[:, inside], scale_bytes[:, inside]
+            words, scale_bytes = (v0, v1_pieces)[g][OUT_COLS.index(cols)]
+            return words[:], scale_bytes[:]
 
         gate_sums = [bank("gate_sums%d" % n, [P, HALF], n) for n in range(len(GATE_COLS))]
         value_sums = [

@@ -32,7 +32,6 @@ KIB = 1024
 ALIGN = 64
 V0_CUT = 288
 G1_CUTS = (slice(0, 96), slice(96, 160), slice(160, 256))
-LAST_CUT = 96
 AT_V0 = 0
 AT_G1 = 8 * KIB
 AT_TURNED = 24 * KIB
@@ -182,12 +181,9 @@ def tile_attend_gatedvalues_heads_kernel(tc, query, keys_words, keys_scales, fac
         nc.vector.reciprocal(out=inv_sum[:], in_=row_sum)
 
         g1_grouped = [None, tile("g1_grouped1", [P, HALF, PACK], BF16)]
-        interleave_on_gpsimd(nc, g1_grouped[1][:, G1_CUTS[0], :], g1_raw[:, :, HALF:E][:, :, G1_CUTS[0]])
-        g0 = [
-            quantise("g0_%d" % h, g0_grouped[:, cols, :], scales_offset=AT_V0 + KIB + HALF * h)
-            for h, cols in enumerate(GATE_COLS)
-        ]
-        v0_third = quantise("v0_1", v0_grouped[:, OUT_COLS[1], :], scales_offset=AT_V0 + 2 * KIB)
+        g0_whole = quantise("g0", g0_grouped[:], offset=AT_V0)
+        g0 = [(g0_whole[0][:, cols], g0_whole[1][:, cols]) for cols in GATE_COLS]
+        interleave_on_vector(nc, g1_grouped[1][:, G1_CUTS[0], :], g1_raw[:, :, HALF:E][:, :, G1_CUTS[0]])
         g1_grouped[0] = tile("g1_grouped0", [P, HALF, PACK], BF16, tag="g0_grouped")
         interleave_on_gpsimd(nc, g1_grouped[0][:], g1_raw[:, :, GATE_COLS[0]])
 
@@ -233,28 +229,27 @@ def tile_attend_gatedvalues_heads_kernel(tc, query, keys_words, keys_scales, fac
         v1_grouped = [
             tile("v1_grouped0", [P, HALF, PACK], BF16, offset=AT_TURNED + ALIGN - 2 * KIB),
             tile("v1_grouped1", [P, QUARTER, PACK], BF16),
-            tile("v1_grouped2", [P, QUARTER, PACK], BF16, offset=AT_TURNED + KIB - ALIGN),
+            tile("v1_grouped2", [P, QUARTER, PACK], BF16),
         ]
-        v1_last = v1_raw[:, :, OUT_COLS[2]]
         interleave_on_scalar(nc, v1_grouped[0][:, 0:QUARTER, :], v1_raw[:, :, 0:QUARTER])
-        interleave_on_scalar(nc, v1_grouped[1][:], v1_raw[:, :, OUT_COLS[1]])
-        interleave_on_scalar(nc, v1_grouped[2][:, 0:LAST_CUT, :], v1_last[:, :, 0:LAST_CUT])
+        for n in (1, 2):
+            interleave_on_scalar(nc, v1_grouped[n][:], v1_raw[:, :, OUT_COLS[n]])
         interleave_on_vector(nc, v1_grouped[0][:, QUARTER:HALF, :], v1_raw[:, :, QUARTER:HALF])
         at = AT_TURNED + ALIGN + HALF
         weights.append(quantise("w1", w_turned[1], scales_offset=at))
         g1.append(quantise("g1_1", g1_grouped[1][:], scales_offset=at + QUARTER))
-        interleave_on_vector(nc, v1_grouped[2][:, LAST_CUT:QUARTER, :], v1_last[:, :, LAST_CUT:QUARTER])
         v1_pieces = [quantise("v1_0", v1_grouped[0][:])]
-        v0.extend((v0_third, quantise("v0_2", v0_grouped[:, OUT_COLS[2], :], scales_offset=at + QUARTER + HALF)))
+        v0_last = quantise("v0_1", v0_grouped[:, GATE_COLS[1], :], scales_offset=at + QUARTER + HALF)
+        v0.extend((v0_last[0][:, cols], v0_last[1][:, cols]) for cols in (slice(0, QUARTER), slice(QUARTER, HALF)))
         v1_pieces.extend(quantise("v1_%d" % n, v1_grouped[n][:]) for n in (1, 2))
 
         def gate_operand(g, cols):
             words, scale_bytes = (g0, g1)[g][GATE_COLS.index(cols)]
-            return words[:], scale_bytes[:]
+            return words[:, :], scale_bytes[:, :]
 
         def value_operand(g, cols):
             words, scale_bytes = (v0, v1_pieces)[g][OUT_COLS.index(cols)]
-            return words[:], scale_bytes[:]
+            return words[:, :], scale_bytes[:, :]
 
         gate_sums = [bank("gate_sums%d" % n, [P, HALF], n) for n in range(len(GATE_COLS))]
         value_sums = [

@@ -222,6 +222,16 @@ def tile_attend_gatedvalues_heads_kernel(tc, query, keys_words, keys_scales, fac
             w_turned.append(turned[:].rearrange("p (q j) -> p q j", j=PACK))
             if g == 0:
                 interleave_on_scalar(nc, g1_grouped[1][:, G1_CUTS[2], :], g1_raw[:, :, HALF:E][:, :, G1_CUTS[2]])
+        unread = bank("unread", [P, K_PASS], 5)
+        nc.tensor.matmul_mx(
+            out=unread[:],
+            lhsT=q_words[:].bitcast(FP8X4),
+            lhsT_scale=q_scales[:],
+            rhs=k_words[:, 0 : 2 * K_PASS].bitcast(FP4X4),
+            rhs_scale=k_scales[:, 0:K_PASS],
+            start=True,
+            stop=True,
+        )
         third_run = AT_V0 + 5 * KIB
         v0 = [quantise("v0_0", v0_grouped[:, GATE_COLS[0], :], scales_offset=third_run)]
         weights = [quantise("w0", w_turned[0])]

@@ -143,21 +143,21 @@ def tile_attend_gatedvalues_heads_kernel(tc, query, keys_words, keys_scales, fac
             else:
                 nc.vector.tensor_copy(out=scores[:, cols], in_=score_sums[:])
 
-        g0_grouped = tile("g0_grouped", [P, E, PACK], BF16)
-        interleave_on_scalar(nc, g0_grouped[:, GATE_COLS[0], :], g0_raw[:, :, GATE_COLS[0]])
-        interleave_on_gpsimd(nc, g0_grouped[:, GATE_COLS[1], :], g0_raw[:, :, GATE_COLS[1]])
-
         columns = SLOTS // PER_COLUMN
         listed = tile("listed", [P, SLOTS], F32)
-        for part in (slice(0, columns // 2), slice(columns // 2, columns)):
-            nc.vector.tensor_copy(
-                out=listed[:, PER_COLUMN * part.start : PER_COLUMN * part.stop], in_=scores[:].indirect(offsets[:, part])
-            )
+        nc.vector.tensor_copy(out=listed[:, 0 : SLOTS // 2], in_=scores[:].indirect(offsets[:, 0 : columns // 2]))
+        nc.scalar.activation(
+            out=listed[:, SLOTS // 2 : SLOTS], in_=scores[:].indirect(offsets[:, columns // 2 : columns]), func=ACT.Copy
+        )
         cut = FIRST // PER_COLUMN
         neg_max = tile("neg_max", [P, 1], F32)
         nc.vector.tensor_copy(out=placed[:].indirect(offsets[:, 0:cut]), in_=listed[:, 0:FIRST])
         nc.vector.tensor_reduce(out=neg_max[:], in_=listed[:], axis=AXIS.X, op=ALU.max, negate=True)
         nc.vector.tensor_copy(out=placed[:].indirect(offsets[:, cut:columns]), in_=listed[:, FIRST:SLOTS])
+
+        g0_grouped = tile("g0_grouped", [P, E, PACK], BF16)
+        interleave_on_scalar(nc, g0_grouped[:, GATE_COLS[0], :], g0_raw[:, :, GATE_COLS[0]])
+        interleave_on_gpsimd(nc, g0_grouped[:, GATE_COLS[1], :], g0_raw[:, :, GATE_COLS[1]])
 
         fac_half = tile("fac_half", [P, PASSES, PACK], F32)
         nc.gpsimd.tensor_scalar(

@@ -35,7 +35,7 @@ G1_CUTS = (slice(0, 96), slice(96, 160), slice(160, 256))
 AT_V0 = 0
 AT_G1 = 8 * KIB
 AT_TURNED = 24 * KIB
-FIRST = 128
+FIRST = 256
 SCORE_COLS = (slice(0, 256), slice(256, 512), slice(512, 768), slice(768, 896), slice(896, 1024))
 GATE_COLS = (slice(0, HALF), slice(HALF, E))
 OUT_COLS = (slice(0, HALF), slice(HALF, HALF + QUARTER), slice(HALF + QUARTER, E))

@@ -35,6 +35,7 @@ G1_CUTS = (slice(0, 96), slice(96, 160), slice(160, 256))
 AT_V0 = 0
 AT_G1 = 8 * KIB
 AT_TURNED = 24 * KIB
+AT_LISTED = 28 * KIB
 FIRST = 256
 SCORE_COLS = (slice(0, 256), slice(256, 512), slice(512, 768), slice(768, 896), slice(896, 1024))
 GATE_COLS = (slice(0, HALF), slice(HALF, E))
@@ -144,7 +145,7 @@ def tile_attend_gatedvalues_heads_kernel(tc, query, keys_words, keys_scales, fac
                 nc.vector.tensor_copy(out=scores[:, cols], in_=score_sums[:])
 
         columns = SLOTS // PER_COLUMN
-        listed = tile("listed", [P, SLOTS], F32)
+        listed = tile("listed", [P, SLOTS], F32, offset=AT_LISTED)
         nc.vector.tensor_copy(out=listed[:, 0 : SLOTS // 2], in_=scores[:].indirect(offsets[:, 0 : columns // 2]))
         nc.scalar.activation(
             out=listed[:, SLOTS // 2 : SLOTS], in_=scores[:].indirect(offsets[:, columns // 2 : columns]), func=ACT.Copy
@@ -178,11 +179,11 @@ def tile_attend_gatedvalues_heads_kernel(tc, query, keys_words, keys_scales, fac
         row_sum = tile("row_sum", [P, 1], F32)[:]
         inv_sum = tile("inv_sum", [P, 1], F32)
         nc.scalar.activation(out=p_listed[:], in_=listed[:], func=ACT.Exp, bias=neg_max[:], accum_out=row_sum)
-        nc.vector.reciprocal(out=inv_sum[:], in_=row_sum)
 
         g1_grouped = [None, tile("g1_grouped1", [P, HALF, PACK], BF16)]
-        g0_whole = quantise("g0", g0_grouped[:], offset=AT_V0)
-        g0 = [(g0_whole[0][:, cols], g0_whole[1][:, cols]) for cols in GATE_COLS]
+        g0 = [quantise("g0_0", g0_grouped[:, GATE_COLS[0], :], scales_offset=AT_V0)]
+        nc.vector.reciprocal(out=inv_sum[:], in_=row_sum)
+        g0.append(quantise("g0_1", g0_grouped[:, GATE_COLS[1], :], scales_offset=AT_LISTED))
         interleave_on_vector(nc, g1_grouped[1][:, G1_CUTS[0], :], g1_raw[:, :, HALF:E][:, :, G1_CUTS[0]])
         g1_grouped[0] = tile("g1_grouped0", [P, HALF, PACK], BF16, tag="g0_grouped")
         interleave_on_gpsimd(nc, g1_grouped[0][:], g1_raw[:, :, GATE_COLS[0]])

@@ -223,16 +223,6 @@ def tile_attend_gatedvalues_heads_kernel(tc, query, keys_words, keys_scales, fac
             w_turned.append(turned[:].rearrange("p (q j) -> p q j", j=PACK))
             if g == 0:
                 interleave_on_scalar(nc, g1_grouped[1][:, G1_CUTS[2], :], g1_raw[:, :, HALF:E][:, :, G1_CUTS[2]])
-        unread = bank("unread", [P, K_PASS], 5)
-        nc.tensor.matmul_mx(
-            out=unread[:],
-            lhsT=q_words[:].bitcast(FP8X4),
-            lhsT_scale=q_scales[:],
-            rhs=k_words[:, 0 : 2 * K_PASS].bitcast(FP4X4),
-            rhs_scale=k_scales[:, 0:K_PASS],
-            start=True,
-            stop=True,
-        )
         third_run = AT_V0 + 5 * KIB
         v0 = [quantise("v0_0", v0_grouped[:, GATE_COLS[0], :], scales_offset=third_run)]
         weights = [quantise("w0", w_turned[0])]

@@ -31,6 +31,7 @@ UNLISTED = -(2.0**127)
 KIB = 1024
 ALIGN = 64
 V0_CUT = 288
+WARM_COLS = 256
 G1_CUTS = (slice(0, 96), slice(96, 160), slice(160, 256))
 AT_V0 = 0
 AT_G1 = 8 * KIB
@@ -223,6 +224,16 @@ def tile_attend_gatedvalues_heads_kernel(tc, query, keys_words, keys_scales, fac
             w_turned.append(turned[:].rearrange("p (q j) -> p q j", j=PACK))
             if g == 0:
                 interleave_on_scalar(nc, g1_grouped[1][:, G1_CUTS[2], :], g1_raw[:, :, HALF:E][:, :, G1_CUTS[2]])
+        unread = bank("unread", [P, WARM_COLS], 5)
+        nc.tensor.matmul_mx(
+            out=unread[:],
+            lhsT=q_words[:].bitcast(FP8X4),
+            lhsT_scale=q_scales[:],
+            rhs=k_words[:, 0 : 2 * WARM_COLS].bitcast(FP4X4),
+            rhs_scale=k_scales[:, 0:WARM_COLS],
+            start=True,
+            stop=True,
+        )
         third_run = AT_V0 + 5 * KIB
         v0 = [quantise("v0_0", v0_grouped[:, GATE_COLS[0], :], scales_offset=third_run)]
         weights = [quantise("w0", w_turned[0])]

@@ -31,6 +31,7 @@ UNLISTED = -(2.0**127)
 KIB = 1024
 ALIGN = 64
 V0_CUT = 288
+FAC_PER_ROW = T // P
 WARM_COLS = 256
 G1_CUTS = (slice(0, 96), slice(96, 160), slice(160, 256))
 AT_V0 = 0
@@ -97,7 +98,7 @@ def tile_attend_gatedvalues_heads_kernel(tc, query, keys_words, keys_scales, fac
         q_raw = tile("q_raw", [P, PACK, Q], F32)
         k_words = tile("k_words", [P, 2 * T], U8)
         k_scales = tile("k_scales", [P, T], U8)
-        fac_raw = tile("fac_raw", [P, PASSES, 2 * PACK], F32)
+        fac_raw = tile("fac_raw", [P, FAC_PER_ROW], F32)
         nc.vector.memset(k_scales[:].bitcast(U32), 0)
         nc.sync.dma_start(out=q_raw[:], in_=query.rearrange("(p j) q -> p j q", j=PACK))
         nc.sync.dma_start(out=k_words[:].bitcast(I32), in_=keys_words[0].bitcast(I32))
@@ -108,7 +109,7 @@ def tile_attend_gatedvalues_heads_kernel(tc, query, keys_words, keys_scales, fac
             )
         nc.sync.dma_start(offsets[:], offs)
         g0_raw = load_pass("g0_raw", gval, 0, slice(0, E))
-        nc.sync.dma_start(out=fac_raw[:, :, 0:PACK], in_=fac.rearrange("o (g p j) -> p (o g) j", g=PASSES, j=PACK))
+        nc.sync.dma_start(out=fac_raw[:], in_=fac.rearrange("o (n i) -> n (o i)", i=FAC_PER_ROW))
         v0_raw = load_pass("v0_raw", vals, 0, slice(0, E), offset=AT_V0)
         g1_raw = load_pass("g1_raw", gval, 1, slice(0, E), offset=AT_G1)
         v1_raw = load_pass("v1_raw", vals, 1, slice(0, E))
@@ -161,16 +162,15 @@ def tile_attend_gatedvalues_heads_kernel(tc, query, keys_words, keys_scales, fac
         interleave_on_scalar(nc, g0_grouped[:, GATE_COLS[0], :], g0_raw[:, :, GATE_COLS[0]])
         interleave_on_gpsimd(nc, g0_grouped[:, GATE_COLS[1], :], g0_raw[:, :, GATE_COLS[1]])
 
-        fac_half = tile("fac_half", [P, PASSES, PACK], F32)
-        nc.gpsimd.tensor_scalar(
-            out=fac_half[:], in0=fac_raw[:, :, 0:PACK], scalar1=0.5, scalar2=0.0, op0=ALU.mult, op1=ALU.add
-        )
+        fac_half = tile("fac_half", [P, FAC_PER_ROW], F32)
+        nc.gpsimd.tensor_scalar(out=fac_half[:], in0=fac_raw[:], scalar1=0.5, scalar2=0.0, op0=ALU.mult, op1=ALU.add)
         fac_rows = []
-        for g in range(PASSES):
-            rows = bank("fac_rows%d" % g, [P, 2, P, 2], 4 + g)
-            for j in range(PACK):
-                nc.tensor.transpose(rows[:, j // 2, :, j % 2], fac_half[:, g, j : j + 1].to_broadcast([P, P]), ident[:])
-            fac_rows.append(rows)
+        for u in range(2):
+            rows = bank("fac_rows%d" % u, [P, P, 2, 2], 4 + u)
+            for b, e in itertools.product(range(2), range(2)):
+                i = PACK * b + 2 * u + e
+                nc.tensor.transpose(rows[:, :, b, e], fac_half[:, i : i + 1].to_broadcast([P, P]), ident[:])
+            fac_rows.append(rows[:].rearrange("q n b e -> q (n b e)"))
 
         v0_grouped = tile("v0_grouped", [P, E, PACK], BF16)
         interleave_on_scalar(nc, v0_grouped[:, 0:V0_CUT, :], v0_raw[:, :, 0:V0_CUT])
@@ -211,7 +211,7 @@ def tile_attend_gatedvalues_heads_kernel(tc, query, keys_words, keys_scales, fac
                     out=run,
                     in0=p_placed[g, u][:],
                     scalar=inv_sum[:],
-                    in1=fac_rows[g][:, u, :, :].rearrange("q p j -> q (p j)"),
+                    in1=fac_rows[u][:, 2 * P * g : 2 * P * (g + 1)],
                     op0=ALU.mult,
                     op1=ALU.mult,
                 )

@@ -102,10 +102,10 @@ def tile_attend_gatedvalues_heads_kernel(tc, query, keys_words, keys_scales, fac
         nc.vector.memset(k_scales[:].bitcast(U32), 0)
         nc.sync.dma_start(out=q_raw[:], in_=query.rearrange("(p j) q -> p j q", j=PACK))
         nc.sync.dma_start(out=k_words[:].bitcast(I32), in_=keys_words[0].bitcast(I32))
-        for quad in range(4):
+        for row in range(4):
             nc.sync.dma_start(
-                out=k_scales[32 * quad : 32 * quad + 4, :].bitcast(I32),
-                in_=keys_scales[0, 4 * quad : 4 * quad + 4, :].bitcast(I32),
+                out=k_scales[row:P:32, :].bitcast(I32),
+                in_=keys_scales[0, row:16:4, :].bitcast(I32),
             )
         nc.sync.dma_start(offsets[:], offs)
         g0_raw = load_pass("g0_raw", gval, 0, slice(0, E))

@@ -24,7 +24,7 @@ PACK = 4
 K_PASS = P * PACK
 PASSES = T // K_PASS
 PER_COLUMN = 16
-LINE = 4
+LINE = 2
 HALF = E // 2
 QUARTER = E // 4
 UNLISTED = -(2.0**127)

import itertools
from contextlib import ExitStack

import concourse.mybir as mybir
from concourse.masks import make_identity

D, T, Q, SLOTS, E = 512, 1024, 128, 512, 512
FLOPS = 2 * Q * D * T + 2 * 2 * Q * T * E

F32 = mybir.dt.float32
BF16 = mybir.dt.bfloat16
I32 = mybir.dt.int32
U32 = mybir.dt.uint32
U16 = mybir.dt.uint16
U8 = mybir.dt.uint8
FP8X4 = mybir.dt.float8_e4m3fn_x4
FP4X4 = mybir.dt.float4_e2m1fn_x4
ALU = mybir.AluOpType
ACT = mybir.ActivationFunctionType
AXIS = mybir.AxisListType

P = 128
PACK = 4
K_PASS = P * PACK
PASSES = T // K_PASS
PER_COLUMN = 16
LINE = 2
HALF = E // 2
QUARTER = E // 4
UNLISTED = -(2.0**127)
KIB = 1024
ALIGN = 64
V0_CUT = 288
FAC_PER_ROW = T // P
WARM_COLS = 256
G1_CUTS = (slice(0, 96), slice(96, 160), slice(160, 256))
AT_V0 = 0
AT_G1 = 8 * KIB
AT_TURNED = 24 * KIB
AT_LISTED = 28 * KIB
FIRST = 256
SCORE_COLS = (slice(0, 256), slice(256, 512), slice(512, 768), slice(768, 896), slice(896, 1024))
GATE_COLS = (slice(0, HALF), slice(HALF, E))
OUT_COLS = (slice(0, HALF), slice(HALF, HALF + QUARTER), slice(HALF + QUARTER, E))


def interleave_views(grouped, raw):
    return (
        grouped.rearrange("p (c i) j -> p c j i", i=LINE),
        raw.rearrange("p j (c i) -> p c j i", i=LINE),
    )


def interleave_on_vector(nc, grouped, raw):
    dst, src = interleave_views(grouped, raw)
    nc.vector.tensor_copy(out=dst, in_=src)


def interleave_on_scalar(nc, grouped, raw):
    dst, src = interleave_views(grouped, raw)
    nc.scalar.activation(out=dst, in_=src, func=ACT.Copy)


def interleave_on_gpsimd(nc, grouped, raw):
    nc.gpsimd.tensor_scalar(out=grouped, in0=raw.rearrange("p j x -> p x j"), scalar1=1.0, scalar2=0.0, op0=ALU.mult, op1=ALU.add)


def tile_attend_gatedvalues_heads_kernel(tc, query, keys_words, keys_scales, fac, vals, gval, offs, out):
    nc = tc.nc
    with ExitStack() as ctx:
        sbuf = ctx.enter_context(tc.tile_pool(name="sbuf", bufs=1))
        shared = ctx.enter_context(tc.tile_pool(name="shared", bufs=1))
        psum = ctx.enter_context(tc.psum_pool(name="psum", bufs=1))

        def tile(name, shape, dtype, tag=None, offset=None):
            if offset is not None:
                return shared.tile(shape, dtype, name=name, align_bytes=64, offset=offset)
            return sbuf.tile(shape, dtype, name=name, tag=tag or name, align_bytes=64)

        def bank(name, shape, number):
            return psum.tile(shape, F32, name=name, tag="bank%d" % number)

        def load_pass(name, source, g, cols, offset=None):
            raw = tile(name, [P, PACK, cols.stop - cols.start], F32, offset=offset)
            rows = source[K_PASS * g : K_PASS * (g + 1), :].rearrange("(p j) e -> p j e", j=PACK)
            nc.sync.dma_start(out=raw[:], in_=rows[:, :, cols])
            return raw

        def quantise(name, grouped, offset=None, scales_offset=None):
            words = tile(name + "_words", [P, grouped.shape[1]], U32, offset=offset)
            scale_bytes = tile(name + "_scales", [P, grouped.shape[1]], U8, offset=scales_offset)
            nc.vector.quantize_mx(
                out=words[:].bitcast(FP8X4), scales=scale_bytes[:], in_=grouped.rearrange("p x j -> p (x j)")
            )
            return words, scale_bytes

        offsets = sbuf.tile([P, SLOTS // PER_COLUMN], U16, name="offsets")
        q_raw = tile("q_raw", [P, PACK, Q], F32)
        k_words = tile("k_words", [P, 2 * T], U8)
        k_scales = tile("k_scales", [P, T], U8)
        fac_raw = tile("fac_raw", [P, FAC_PER_ROW], F32)
        nc.vector.memset(k_scales[:].bitcast(U32), 0)
        nc.sync.dma_start(out=q_raw[:], in_=query.rearrange("(p j) q -> p j q", j=PACK))
        nc.sync.dma_start(out=k_words[:].bitcast(I32), in_=keys_words[0].bitcast(I32))
        for row in range(4):
            nc.sync.dma_start(
                out=k_scales[row:P:32, :].bitcast(I32),
                in_=keys_scales[0, row:16:4, :].bitcast(I32),
            )
        nc.sync.dma_start(offsets[:], offs)
        g0_raw = load_pass("g0_raw", gval, 0, slice(0, E))
        nc.sync.dma_start(out=fac_raw[:], in_=fac.rearrange("o (n i) -> n (o i)", i=FAC_PER_ROW))
        v0_raw = load_pass("v0_raw", vals, 0, slice(0, E), offset=AT_V0)
        g1_raw = load_pass("g1_raw", gval, 1, slice(0, E), offset=AT_G1)
        v1_raw = load_pass("v1_raw", vals, 1, slice(0, E))

        ident = tile("ident", [P, P], F32)
        nc.vector.memset(ident[:], 0.0)
        make_identity(nc, ident[:], nomemset=True)
        placed = tile("placed", [P, T], F32)
        nc.vector.memset(placed[:], UNLISTED)

        q_grouped = tile("q_grouped", [P, Q, PACK], BF16)
        q_words = tile("q_words", [P, Q], U32)
        q_scales = tile("q_scales", [P, Q], U8)
        q_halves = (slice(0, Q // 2), slice(Q // 2, Q))
        interleave_on_vector(nc, q_grouped[:, q_halves[0], :], q_raw[:, :, q_halves[0]])
        interleave_on_scalar(nc, q_grouped[:, q_halves[1], :], q_raw[:, :, q_halves[1]])
        nc.vector.quantize_mx(
            out=q_words[:].bitcast(FP8X4), scales=q_scales[:], in_=q_grouped[:].rearrange("p q j -> p (q j)")
        )
        scores = tile("scores", [P, T], F32)
        for n, cols in enumerate(SCORE_COLS):
            score_sums = bank("score_sums%d" % n, [P, cols.stop - cols.start], (n + 6) % 8)
            nc.tensor.matmul_mx(
                out=score_sums[:],
                lhsT=q_words[:].bitcast(FP8X4),
                lhsT_scale=q_scales[:],
                rhs=k_words[:, 2 * cols.start : 2 * cols.stop].bitcast(FP4X4),
                rhs_scale=k_scales[:, cols],
                start=True,
                stop=True,
            )
            if n % 2 == 0:
                nc.scalar.activation(out=scores[:, cols], in_=score_sums[:], func=ACT.Copy)
            else:
                nc.vector.tensor_copy(out=scores[:, cols], in_=score_sums[:])

        columns = SLOTS // PER_COLUMN
        listed = tile("listed", [P, SLOTS], F32, offset=AT_LISTED)
        nc.vector.tensor_copy(out=listed[:, 0 : SLOTS // 2], in_=scores[:].indirect(offsets[:, 0 : columns // 2]))
        nc.scalar.activation(
            out=listed[:, SLOTS // 2 : SLOTS], in_=scores[:].indirect(offsets[:, columns // 2 : columns]), func=ACT.Copy
        )
        cut = FIRST // PER_COLUMN
        neg_max = tile("neg_max", [P, 1], F32)
        nc.vector.tensor_copy(out=placed[:].indirect(offsets[:, 0:cut]), in_=listed[:, 0:FIRST])
        nc.vector.tensor_reduce(out=neg_max[:], in_=listed[:], axis=AXIS.X, op=ALU.max, negate=True)
        nc.vector.tensor_copy(out=placed[:].indirect(offsets[:, cut:columns]), in_=listed[:, FIRST:SLOTS])

        g0_grouped = tile("g0_grouped", [P, E, PACK], BF16)
        interleave_on_scalar(nc, g0_grouped[:, GATE_COLS[0], :], g0_raw[:, :, GATE_COLS[0]])
        interleave_on_gpsimd(nc, g0_grouped[:, GATE_COLS[1], :], g0_raw[:, :, GATE_COLS[1]])

        fac_half = tile("fac_half", [P, FAC_PER_ROW], F32)
        nc.gpsimd.tensor_scalar(out=fac_half[:], in0=fac_raw[:], scalar1=0.5, scalar2=0.0, op0=ALU.mult, op1=ALU.add)
        fac_rows = []
        for u in range(2):
            rows = bank("fac_rows%d" % u, [P, P, 2, 2], 4 + u)
            for b, e in itertools.product(range(2), range(2)):
                i = PACK * b + 2 * u + e
                nc.tensor.transpose(rows[:, :, b, e], fac_half[:, i : i + 1].to_broadcast([P, P]), ident[:])
            fac_rows.append(rows[:].rearrange("q n b e -> q (n b e)"))

        v0_grouped = tile("v0_grouped", [P, E, PACK], BF16)
        interleave_on_scalar(nc, v0_grouped[:, 0:V0_CUT, :], v0_raw[:, :, 0:V0_CUT])
        interleave_on_gpsimd(nc, v0_grouped[:, V0_CUT:E, :], v0_raw[:, :, V0_CUT:E])

        p_listed = tile("p_listed", [P, SLOTS], F32, offset=AT_V0 + KIB)
        row_sum = tile("row_sum", [P, 1], F32)[:]
        inv_sum = tile("inv_sum", [P, 1], F32)
        nc.scalar.activation(out=p_listed[:], in_=listed[:], func=ACT.Exp, bias=neg_max[:], accum_out=row_sum)

        g1_grouped = [None, tile("g1_grouped1", [P, HALF, PACK], BF16)]
        g0 = [quantise("g0_0", g0_grouped[:, GATE_COLS[0], :], scales_offset=AT_V0)]
        nc.vector.reciprocal(out=inv_sum[:], in_=row_sum)
        g0.append(quantise("g0_1", g0_grouped[:, GATE_COLS[1], :], scales_offset=AT_LISTED))
        interleave_on_vector(nc, g1_grouped[1][:, G1_CUTS[0], :], g1_raw[:, :, HALF:E][:, :, G1_CUTS[0]])
        g1_grouped[0] = tile("g1_grouped0", [P, HALF, PACK], BF16, tag="g0_grouped")
        interleave_on_gpsimd(nc, g1_grouped[0][:], g1_raw[:, :, GATE_COLS[0]])

        p_placed = {}
        for g, u in itertools.product(range(PASSES), range(2)):
            p_placed[g, u] = tile("p_placed%d%d" % (g, u), [P, 2 * P], F32, offset=AT_V0 + (3 + 2 * g + u) * KIB)
            tokens = placed[:, K_PASS * g : K_PASS * (g + 1)].rearrange("q (p j) -> q p j", j=PACK)
            nc.scalar.activation(
                out=p_placed[g, u][:].rearrange("q (p j) -> q p j", j=2),
                in_=tokens[:, :, 2 * u : 2 * u + 2],
                func=ACT.Exp,
                bias=neg_max[:],
            )
        interleave_on_scalar(nc, g1_grouped[1][:, G1_CUTS[1], :], g1_raw[:, :, HALF:E][:, :, G1_CUTS[1]])

        w_turned = []
        for g in range(PASSES):
            w_pairs = tile("w_pairs%d" % g, [P, K_PASS], BF16)
            turned_words = bank("turned_words%d" % g, [P, 2, Q], 6 + g)
            for u in range(2):
                run = w_pairs[:, 2 * P * u : 2 * P * (u + 1)]
                nc.vector.scalar_tensor_tensor(
                    out=run,
                    in0=p_placed[g, u][:],
                    scalar=inv_sum[:],
                    in1=fac_rows[u][:, 2 * P * g : 2 * P * (g + 1)],
                    op0=ALU.mult,
                    op1=ALU.mult,
                )
                nc.tensor.transpose(turned_words[:, u, :], run.bitcast(F32), ident[:])
            turned = tile("w_turned%d" % g, [P, Q * PACK], BF16, offset=AT_TURNED + 2 * KIB * g)
            nc.scalar.copy(
                out=turned[:].bitcast(F32).rearrange("p (q u) -> p q u", u=2),
                in_=turned_words[:].rearrange("p u q -> p q u"),
            )
            w_turned.append(turned[:].rearrange("p (q j) -> p q j", j=PACK))
            if g == 0:
                interleave_on_scalar(nc, g1_grouped[1][:, G1_CUTS[2], :], g1_raw[:, :, HALF:E][:, :, G1_CUTS[2]])
        unread = bank("unread", [P, WARM_COLS], 5)
        nc.tensor.matmul_mx(
            out=unread[:],
            lhsT=q_words[:].bitcast(FP8X4),
            lhsT_scale=q_scales[:],
            rhs=k_words[:, 0 : 2 * WARM_COLS].bitcast(FP4X4),
            rhs_scale=k_scales[:, 0:WARM_COLS],
            start=True,
            stop=True,
        )
        third_run = AT_V0 + 5 * KIB
        v0 = [quantise("v0_0", v0_grouped[:, GATE_COLS[0], :], scales_offset=third_run)]
        weights = [quantise("w0", w_turned[0])]
        g1 = [quantise("g1_0", g1_grouped[0][:], scales_offset=AT_TURNED + ALIGN)]
        v1_grouped = [
            tile("v1_grouped0", [P, HALF, PACK], BF16, offset=AT_TURNED + ALIGN - 2 * KIB),
            tile("v1_grouped1", [P, QUARTER, PACK], BF16),
            tile("v1_grouped2", [P, QUARTER, PACK], BF16),
        ]
        interleave_on_scalar(nc, v1_grouped[0][:, 0:QUARTER, :], v1_raw[:, :, 0:QUARTER])
        for n in (1, 2):
            interleave_on_scalar(nc, v1_grouped[n][:], v1_raw[:, :, OUT_COLS[n]])
        interleave_on_vector(nc, v1_grouped[0][:, QUARTER:HALF, :], v1_raw[:, :, QUARTER:HALF])
        at = AT_TURNED + ALIGN + HALF
        weights.append(quantise("w1", w_turned[1], scales_offset=at))
        g1.append(quantise("g1_1", g1_grouped[1][:], scales_offset=at + QUARTER))
        v1_pieces = [quantise("v1_0", v1_grouped[0][:])]
        v0_last = quantise("v0_1", v0_grouped[:, GATE_COLS[1], :], scales_offset=at + QUARTER + HALF)
        v0.extend((v0_last[0][:, cols], v0_last[1][:, cols]) for cols in (slice(0, QUARTER), slice(QUARTER, HALF)))
        v1_pieces.extend(quantise("v1_%d" % n, v1_grouped[n][:]) for n in (1, 2))

        def gate_operand(g, cols):
            words, scale_bytes = (g0, g1)[g][GATE_COLS.index(cols)]
            return words[:, :], scale_bytes[:, :]

        def value_operand(g, cols):
            words, scale_bytes = (v0, v1_pieces)[g][OUT_COLS.index(cols)]
            return words[:, :], scale_bytes[:, :]

        gate_sums = [bank("gate_sums%d" % n, [P, HALF], n) for n in range(len(GATE_COLS))]
        value_sums = [
            bank("value_sums%d" % n, [P, cols.stop - cols.start], len(GATE_COLS) + n) for n, cols in enumerate(OUT_COLS)
        ]
        products = [(gate_sums[n], gate_operand, cols) for n, cols in enumerate(GATE_COLS)]
        products.extend((value_sums[n], value_operand, cols) for n, cols in enumerate(OUT_COLS))
        runs = (products[:2], products[2:3], products[3:4], products[4:])
        for run, g in itertools.product(runs, range(PASSES)):
            for sums, operand, cols in run:
                words, scale_bytes = operand(g, cols)
                nc.tensor.matmul_mx(
                    out=sums[:],
                    lhsT=weights[g][0][:].bitcast(FP8X4),
                    lhsT_scale=weights[g][1][:],
                    rhs=words.bitcast(FP8X4),
                    rhs_scale=scale_bytes,
                    start=(g == 0),
                    stop=(g == PASSES - 1),
                )

        gate = tile("gate", [P, E], F32)
        for n, cols in enumerate(GATE_COLS):
            nc.scalar.activation(out=gate[:, cols], in_=gate_sums[n][:], func=ACT.Tanh)
        for n, cols in enumerate(OUT_COLS):
            result = tile("result%d" % n, [P, cols.stop - cols.start], F32)
            nc.vector.scalar_tensor_tensor(
                out=result[:], in0=gate[:, cols], scalar=1.0, in1=value_sums[n][:], op0=ALU.add, op1=ALU.mult
            )
            nc.sync.dma_start(out=out[:, cols], in_=result[:])
